import numpy as np
import ml_dtypes


def mxq(x, axis, fmt="e4m3"):
    dtype, down = {"e4m3": (ml_dtypes.float8_e4m3fn, 7), "e5m2": (ml_dtypes.float8_e5m2, 14)}[fmt]
    v = np.moveaxis(np.asarray(x, np.float32).astype(ml_dtypes.bfloat16).astype(np.float64), axis, -1)
    blocks = v.reshape(v.shape[:-1] + (-1, 32))
    amax = np.abs(blocks).max(-1, keepdims=True)
    byte = np.maximum(np.where(amax > 0, np.frexp(amax)[1] - 1 + 127, 0) - down, 1)
    scale = np.exp2(byte - 127.0)
    codes = (blocks / scale).astype(np.float32).astype(dtype).astype(np.float64)
    return np.moveaxis((codes * scale).reshape(v.shape), -1, axis)


WIDE = False


def mx_kscale(k):
    if not WIDE:
        return np.ones(k)
    levels = np.array([10, -10, 5, -5, 0])
    if k % 512:
        return np.exp2(np.random.permutation(np.resize(levels, k // 32))).repeat(32)
    a = np.empty((k // 512, 16))
    for p in range(k // 512):
        a[p, :8] = np.random.permutation(np.resize(levels, 8))
        for g in range(8):
            far = levels[np.abs(levels - a[p, g]) >= 10]
            a[p, g + 8] = far[np.random.randint(len(far))]
    return np.exp2(a.ravel()).repeat(32)


def f64(x):
    return np.asarray(x).astype(np.float64)


def striped(idx):
    return np.tile(idx.reshape(-1, 16).T, (8, 1)).astype(np.uint16)


def unstriped(offs):
    return offs[:16].T.reshape(-1).astype(np.int64)


def pack_weight(w):
    k, n = w.shape
    w = f64(np.asarray(w, np.float32).astype(ml_dtypes.bfloat16)).reshape(k // 32, 32, n)
    amax = np.abs(w).max(1)
    byte = np.clip(np.where(amax > 0, np.frexp(amax)[1] - 1 + 127 - 7, 1), 1, 254)
    scaled = (w * np.exp2(127.0 - byte)[:, None, :]).reshape(k, n).astype(np.float32)
    words = np.ascontiguousarray(scaled.reshape(k // 512, 128, 4, n).transpose(0, 1, 3, 2)).astype(ml_dtypes.float8_e4m3fn).view(np.uint8)
    return words, np.ascontiguousarray(byte.astype(np.uint8).reshape(k // 512, 16, n))


def unpack_weight(words, scales):
    g, p, n, _ = words.shape
    vals = np.ascontiguousarray(words).view(ml_dtypes.float8_e4m3fn).astype(np.float64) * np.repeat(np.exp2(scales.astype(np.float64) - 127.0), 8, axis=1)[..., None]
    return vals.transpose(0, 1, 3, 2).reshape(g * 512, n)


def planes(y):
    n, m = y.shape
    v = y.astype(np.float32).astype(ml_dtypes.bfloat16).astype(np.float64).reshape(n // 32, 32, m)
    top = np.abs(v).max(1)
    byte = np.clip(np.where(top > 0, np.frexp(top)[1] - 1 + 127 - 7, 1), 1, 254)
    codes = (v * np.exp2(127.0 - byte)[:, None, :]).reshape(n, m).astype(np.float32).astype(ml_dtypes.float8_e4m3fn).view(np.uint8)
    words = codes.reshape(n // 512, 128, 4, m).transpose(0, 1, 3, 2)
    return np.ascontiguousarray(words), np.ascontiguousarray(byte.astype(np.uint8).reshape(n // 512, 16, m))


def relu(v):
    return np.maximum(v, 0.0)


K, T, S, H, N, D = 512, 1024, 512, 512, 512, 2
P = 2 ** 7


def setup_inputs():
    n = np.random.standard_normal
    s = mx_kscale(K)[:, None]
    u = mx_kscale(H)
    packed_xT = pack_weight(n((K, T)) * s)
    return {
        "x_words": packed_xT[0],
        "x_scales": packed_xT[1],
        "w1": (n((K, H)) / np.sqrt(K) / s * u).astype(np.float32),
        "w2": (n((H, N)) / np.sqrt(H) / u[:, None]).astype(np.float32),
        "kern": (np.tile(0.7 * n((D, 1, S)), (1, P, 1))).astype(np.float32),
        "cur": (n((N, S))).astype(np.float32),
        "fire": (np.tile((np.random.uniform(size=S) < 0.5) * 1.0, (P, 1))).astype(np.float32),
        "offs": striped(np.random.permutation(T)[:S]),
        "pos1": striped(np.random.permutation(S)[:S]),
        "pos2": striped(np.random.permutation(S)[:S]),
    }


def reference(x_words, x_scales, w1, w2, kern, cur, fire, offs, pos1, pos2):
    xq = unpack_weight(x_words, x_scales)[:, unstriped(offs)]
    y = mxq(f64(w1), 0, "e4m3").T @ xq
    h = relu(y + y[:, unstriped(pos1)] * f64(kern)[0, :1] + y[:, unstriped(pos2)] * f64(kern)[1, :1])
    rr = mxq(f64(w2), 0, "e4m3").T @ mxq(h, 0, "e4m3")
    out_0 = f64(cur) + rr * f64(fire)[:1]
    return (out_0,) + planes(out_0)

@@ -1,0 +1,199 @@
+from contextlib import ExitStack
+
+import concourse.mybir as mybir
+from concourse.masks import make_identity
+
+K, T, S, H, N = 512, 1024, 512, 512, 512
+FLOPS = 2 * K * H * S + 2 * H * N * S
+
+F32 = mybir.dt.float32
+BF16 = mybir.dt.bfloat16
+I32 = mybir.dt.int32
+U32 = mybir.dt.uint32
+U16 = mybir.dt.uint16
+U8 = mybir.dt.uint8
+FP8X4 = mybir.dt.float8_e4m3fn_x4
+MULT = mybir.AluOpType.mult
+ADD = mybir.AluOpType.add
+RELU = mybir.ActivationFunctionType.Relu
+
+P = 128
+PACK = 4
+CHUNKS = [(0, 384), (384, 128)]
+W1_LOADS = [(0, 128), (128, 128), (256, 256)]
+
+
+def tile_picked_ynca_add_po_kernel(
+    tc, x_words, x_scales, w1, w2, kern, cur, fire, offs, pos1, pos2, out_0, out_1, out_2
+):
+    nc = tc.nc
+    with ExitStack() as ctx:
+        lists = ctx.enter_context(tc.tile_pool(name="lists", bufs=1))
+        keep = ctx.enter_context(tc.tile_pool(name="keep", bufs=1))
+        psum = ctx.enter_context(tc.psum_pool(name="psum", bufs=1))
+
+        offs_sb = lists.tile([P, S // 16], U16, name="offs_sb")
+        pos_sb = [lists.tile([P, S // 16], U16, name="pos_sb%d" % d) for d in range(2)]
+
+        nc.sync.dma_start(offs_sb[:], offs)
+        xs = keep.tile([P, T], U8, name="xs", align_bytes=64)
+        nc.gpsimd.memset(xs[:].bitcast(I32), 0)
+        for q in range(4):
+            queue = nc.scalar if q < 2 else nc.sync
+            queue.dma_start(xs[32 * q : 32 * q + 4, :].bitcast(I32), x_scales[0, 4 * q : 4 * q + 4, :].bitcast(I32))
+        xw = keep.tile([P, T], U32, name="xw", align_bytes=64)
+
+        w1_rows = w1.rearrange("(p j) c -> p j c", j=PACK)
+        w1_raw = []
+        kern_sb = keep.tile([P, 2, S], F32, name="kern_sb")
+        for n, (c0, width) in enumerate(W1_LOADS):
+            raw = keep.tile([P, PACK, width], F32, name="w1_raw%d" % n)
+            nc.sync.dma_start(raw[:], w1_rows[:, :, c0 : c0 + width])
+            for a0 in range(0, width, P):
+                w1_raw.append(raw[:, :, a0 : a0 + P])
+            if n == 0:
+                nc.sync.dma_start(xw[:].bitcast(I32), x_words[0].rearrange("p c r -> p (c r)").bitcast(I32))
+            if n == 1:
+                nc.sync.dma_start(kern_sb[:], kern.rearrange("d p j -> p d j"))
+                nc.sync.dma_start(pos_sb[0][:], pos1)
+                nc.sync.dma_start(pos_sb[1][:], pos2)
+        w2_raw = keep.tile([P, PACK, N], F32, name="w2_raw")
+        nc.sync.dma_start(w2_raw[:], w2.rearrange("(p j) c -> p j c", j=PACK))
+        fire_col = keep.tile([P, S // P], F32, name="fire_col")
+        with nc.allow_non_contiguous_dma(reason="one value a partition"):
+            nc.sync.dma_start(fire_col[:], fire[0].rearrange("(b p) -> p b", p=P))
+        cur_sb = keep.tile([P, PACK, S], F32, name="cur_sb")
+        nc.sync.dma_start(cur_sb[:], cur.rearrange("(p t) j -> p t j", t=PACK))
+
+        ident = keep.tile([P, P], F32, name="ident")
+        make_identity(nc, ident[:])
+
+        gs = keep.tile([P, S], U8, name="gs", align_bytes=64)
+        nc.vector.tensor_copy(gs[:], xs[:].indirect(offs_sb[:]))
+        half = S // 2
+        gw = [keep.tile([P, half], U32, name="gw%d" % n, align_bytes=64) for n in range(2)]
+
+        y = []
+        for a in range(H // P):
+            grouped = keep.tile([P, P, PACK], BF16, name="w1_bf%d" % a, align_bytes=64)
+            nc.scalar.copy(
+                grouped[:].rearrange("p (c i) t -> p c t i", i=4),
+                w1_raw[a].rearrange("p t (c i) -> p c t i", i=4),
+            )
+            codes = keep.tile([P, P], U32, name="w1_codes%d" % a, align_bytes=64)
+            scales = keep.tile([P, P], U8, name="w1_scales%d" % a, align_bytes=64)
+            nc.vector.quantize_mx(codes[:].bitcast(FP8X4), scales[:], grouped[:].rearrange("p c t -> p (c t)"))
+            y_a = keep.tile([P, S], F32, name="y%d" % a)
+            for n in range(2):
+                cols = slice(n * half, (n + 1) * half)
+                if a == 0:
+                    nc.vector.tensor_copy(gw[n][:], xw[:].indirect(offs_sb[:, n * half // 16 : (n + 1) * half // 16]))
+                if a == 0 or n == 0:
+                    bank = psum.tile([P, S], F32, name="ybank", tag="acc", bufs=2)
+                nc.tensor.matmul_mx(bank[:, cols], codes[:].bitcast(FP8X4), scales[:], gw[n][:].bitcast(FP8X4), gs[:, cols], start=True, stop=True)
+                if a == 0 and n == 0:
+                    nc.scalar.copy(y_a[:, cols], bank[:, cols])
+                if a == 0 and n == 1:
+                    nc.vector.tensor_copy(y_a[:, cols], bank[:, cols])
+            if a > 0:
+                nc.scalar.copy(y_a[:], bank[:])
+            y.append(y_a)
+
+        w2_bf = keep.tile([P, PACK, P, PACK], BF16, name="w2_bf", align_bytes=64)
+        w2_codes = keep.tile([P, N], U32, name="w2_codes", align_bytes=64)
+        w2_scales = keep.tile([P, N], U8, name="w2_scales", align_bytes=64)
+
+        def quantise_w2():
+            for m0 in range(0, P, 32):
+                nc.scalar.copy(
+                    w2_bf[:].rearrange("p t m j -> p m j t")[:, m0 : m0 + 32],
+                    w2_raw[:].rearrange("p j (m t) -> p m j t", t=PACK)[:, m0 : m0 + 32],
+                )
+            nc.vector.quantize_mx(w2_codes[:].bitcast(FP8X4), w2_scales[:], w2_bf[:].rearrange("p t m j -> p (t m j)"))
+
+        out_codes = keep.tile([P, S], U32, name="out_codes", align_bytes=64)
+        out_scales = keep.tile([P, S], U8, name="out_scales", align_bytes=64)
+        out_rows = out_0.rearrange("(p t) j -> p t j", t=PACK)
+        out_words = out_1[0].rearrange("p c r -> p (c r)").bitcast(I32)
+
+        blocks = S // P
+        hT_bank = [psum.tile([P, H], F32, name="hT%d" % jb) for jb in range(blocks)]
+        hT_bf = [keep.tile([P, H], BF16, name="hT_bf%d" % jb) for jb in range(blocks)]
+
+        def perceive(j0, width, a, regions):
+            terms = [y[a][:, j0 : j0 + width]]
+            for d in range(2):
+                g = keep.tile([P, width], F32, name="g", bufs=4)
+                nc.vector.tensor_tensor(
+                    g[:],
+                    y[a][:].indirect(pos_sb[d][:, j0 // 16 : (j0 + width) // 16]),
+                    kern_sb[:, d, j0 : j0 + width],
+                    MULT,
+                )
+                terms.append(g[:])
+            for n, term in enumerate(terms):
+                for b, region in enumerate(regions):
+                    nc.tensor.matmul(region, term[:, b * P : (b + 1) * P], ident[:], start=(n == 0), stop=(n == 2), is_transpose=True)
+
+        def activate(jb, source, a0, a1):
+            nc.scalar.activation(
+                hT_bf[jb][:].rearrange("j (u p e) -> j u p e", u=2, e=2)[:, :, 32 * a0 : 32 * a1, :],
+                source.rearrange("j (p u e) -> j u p e", u=2, e=2),
+                RELU,
+                scale=fire_col[:, jb : jb + 1],
+            )
+
+        h_mx = dict()
+
+        def quantise_h(jb):
+            hT = hT_bf[jb]
+            words = hT[:].bitcast(F32)
+            back = psum.tile([P, 2, P], F32, name="back", bufs=2)
+            for u in range(2):
+                nc.tensor.transpose(back[:, u, :], words[:, u * P : (u + 1) * P], ident[:])
+            h_bf = keep.tile([P, P * PACK], BF16, name="h_bf%d" % jb, align_bytes=64)
+            nc.scalar.copy(h_bf[:].bitcast(F32).rearrange("p (j u) -> p j u", u=2), back[:].rearrange("p u j -> p j u"))
+            h_codes = keep.tile([P, P], U32, name="h_codes%d" % jb, align_bytes=64)
+            h_scales = keep.tile([P, P], U8, name="h_scales%d" % jb, align_bytes=64)
+            nc.vector.quantize_mx(h_codes[:].bitcast(FP8X4), h_scales[:], h_bf[:])
+            h_mx.setdefault(jb, (h_codes, h_scales))
+
+        def update(jb):
+            cols = slice(jb * P, (jb + 1) * P)
+            h_codes, h_scales = h_mx[jb]
+            rr = psum.tile([P, PACK, P], F32, name="rr", tag="acc", bufs=2)
+            for t in range(PACK):
+                m = slice(t * P, (t + 1) * P)
+                nc.tensor.matmul_mx(
+                    rr[:, t, :], w2_codes[:, m].bitcast(FP8X4), w2_scales[:, m], h_codes[:].bitcast(FP8X4), h_scales[:], start=True, stop=True
+                )
+            new = keep.tile([P, PACK, P], F32, name="new%d" % jb)
+            nc.vector.tensor_tensor(new[:], rr[:], cur_sb[:, :, cols], ADD)
+            nc.sync.dma_start(out_rows[:, :, cols], new[:])
+            new_bf = keep.tile([P, P, PACK], BF16, name="new_bf%d" % jb, align_bytes=64)
+            nc.scalar.copy(
+                new_bf[:].rearrange("p (c i) t -> p c t i", i=4),
+                new[:].rearrange("p t (c i) -> p c t i", i=4),
+            )
+            nc.vector.quantize_mx(out_codes[:, cols].bitcast(FP8X4), out_scales[:, cols], new_bf[:].rearrange("p c t -> p (c t)"))
+            nc.sync.dma_start(out_words[:, cols], out_codes[:, cols].bitcast(I32))
+
+        last = blocks - 1
+        for a in range(4):
+            perceive(0, last * P, a, [hT_bank[jb][:, a * P : (a + 1) * P] for jb in range(last)])
+        quantise_w2()
+        for jb in range(last):
+            activate(jb, hT_bank[jb][:], 0, 4)
+            quantise_h(jb)
+        for a in range(3):
+            perceive(last * P, P, a, [hT_bank[last][:, a * P : (a + 1) * P]])
+        activate(last, hT_bank[last][:, 0 : 3 * P], 0, 3)
+        spare = psum.tile([P, P], F32, name="hT0")
+        perceive(last * P, P, 3, [spare[:]])
+        activate(last, spare[:], 3, 4)
+        quantise_h(last)
+        for jb in range(blocks):
+            update(jb)
+        for q in range(4):
+            queue = nc.sync if q % 2 else nc.scalar
+            queue.dma_start(out_2[0, 4 * q : 4 * q + 4, :].bitcast(I32), out_scales[32 * q : 32 * q + 4, :].bitcast(I32))

@@ -71,9 +71,12 @@ def tile_picked_ynca_add_po_kernel(
         gs = keep.tile([P, S], U8, name="gs", align_bytes=64)
         nc.vector.tensor_copy(gs[:], xs[:].indirect(offs_sb[:]))
         half = S // 2
-        gw = [keep.tile([P, half], U32, name="gw%d" % n, align_bytes=64) for n in range(2)]
+        gw = []
+        blocks = S // P
+        last = blocks - 1
 
         y = []
+        w1_mx = []
         for a in range(H // P):
             grouped = keep.tile([P, P, PACK], BF16, name="w1_bf%d" % a, align_bytes=64)
             nc.scalar.copy(
@@ -83,47 +86,60 @@ def tile_picked_ynca_add_po_kernel(
             codes = keep.tile([P, P], U32, name="w1_codes%d" % a, align_bytes=64)
             scales = keep.tile([P, P], U8, name="w1_scales%d" % a, align_bytes=64)
             nc.vector.quantize_mx(codes[:].bitcast(FP8X4), scales[:], grouped[:].rearrange("p c t -> p (c t)"))
-            y_a = keep.tile([P, S], F32, name="y%d" % a)
+            w1_mx.append((codes, scales))
+            if a == 0:
+                y_a = keep.tile([P, S], F32, name="y0")
+                for n in range(2):
+                    cols = slice(n * half, (n + 1) * half)
+                    gw.append(keep.tile([P, half], U32, name=("gw0", "w1_bf0")[n], align_bytes=64))
+                    nc.vector.tensor_copy(gw[n][:], xw[:].indirect(offs_sb[:, n * half // 16 : (n + 1) * half // 16]))
+                    bank = psum.tile([P, half], F32, name="ybank", tag="acc", bufs=2)
+                    nc.tensor.matmul_mx(bank[:], codes[:].bitcast(FP8X4), scales[:], gw[n][:].bitcast(FP8X4), gs[:, cols], start=True, stop=True)
+                    copy = nc.vector.tensor_copy if n else nc.scalar.copy
+                    copy(y_a[:, cols], bank[:])
+                y.append(y_a)
+        for a in range(1, H // P):
+            codes, scales = w1_mx[a]
+            bank = psum.tile([P, S], F32, name="hT%d" % (a - 1))
             for n in range(2):
                 cols = slice(n * half, (n + 1) * half)
-                if a == 0:
-                    nc.vector.tensor_copy(gw[n][:], xw[:].indirect(offs_sb[:, n * half // 16 : (n + 1) * half // 16]))
-                if a == 0 or n == 0:
-                    bank = psum.tile([P, S], F32, name="ybank", tag="acc", bufs=2)
                 nc.tensor.matmul_mx(bank[:, cols], codes[:].bitcast(FP8X4), scales[:], gw[n][:].bitcast(FP8X4), gs[:, cols], start=True, stop=True)
-                if a == 0 and n == 0:
-                    nc.scalar.copy(y_a[:, cols], bank[:, cols])
-                if a == 0 and n == 1:
-                    nc.vector.tensor_copy(y_a[:, cols], bank[:, cols])
-            if a > 0:
-                nc.scalar.copy(y_a[:], bank[:])
+            y_a = keep.tile([P, S], F32, name="w1_raw2" if a == 1 else "y%d" % a)
+            nc.scalar.copy(y_a[:], bank[:])
             y.append(y_a)
+        hT_bank = [psum.tile([P, H], F32, name="hT%d" % jb) for jb in range(blocks)]
+        for a in range(H // P):
+            for jb in range(blocks if a < 3 else last):
+                nc.tensor.matmul(
+                    hT_bank[jb][:, a * P : (a + 1) * P], y[a][:, jb * P : (jb + 1) * P], ident[:], start=(a == 0), stop=False, is_transpose=True
+                )
 
         w2_bf = keep.tile([P, PACK, P, PACK], BF16, name="w2_bf", align_bytes=64)
-        w2_codes = keep.tile([P, N], U32, name="w2_codes", align_bytes=64)
         w2_scales = keep.tile([P, N], U8, name="w2_scales", align_bytes=64)
 
         def quantise_w2():
-            for m0 in range(0, P, 32):
-                nc.scalar.copy(
-                    w2_bf[:].rearrange("p t m j -> p m j t")[:, m0 : m0 + 32],
-                    w2_raw[:].rearrange("p j (m t) -> p m j t", t=PACK)[:, m0 : m0 + 32],
-                )
+            w2_codes = keep.tile([P, N], U32, name="w2_codes", align_bytes=64)
+            for t in range(PACK):
+                nc.scalar.copy(w2_bf[:, t], w2_raw[:].rearrange("p j (m t) -> p t m j", t=PACK)[:, t])
             nc.vector.quantize_mx(w2_codes[:].bitcast(FP8X4), w2_scales[:], w2_bf[:].rearrange("p t m j -> p (t m j)"))
+            return w2_codes
 
         out_codes = keep.tile([P, S], U32, name="out_codes", align_bytes=64)
         out_scales = keep.tile([P, S], U8, name="out_scales", align_bytes=64)
         out_rows = out_0.rearrange("(p t) j -> p t j", t=PACK)
         out_words = out_1[0].rearrange("p c r -> p (c r)").bitcast(I32)
 
-        blocks = S // P
-        hT_bank = [psum.tile([P, H], F32, name="hT%d" % jb) for jb in range(blocks)]
         hT_bf = [keep.tile([P, H], BF16, name="hT_bf%d" % jb) for jb in range(blocks)]
 
-        def perceive(j0, width, a, regions):
-            terms = [y[a][:, j0 : j0 + width]]
+        def perceive(j0, width, a, regions, closes):
+            terms = []
             for d in range(2):
-                g = keep.tile([P, width], F32, name="g", bufs=4)
+                if j0 == 0 and 2 * a + d in (1, 2):
+                    g = keep.tile([P, width], F32, name="w1_bf%d" % (2 * a + d + 1), align_bytes=64)
+                elif j0 == 0 and 2 * a + d == 6:
+                    g = keep.tile([P, width], F32, name="w2_codes", align_bytes=64)
+                else:
+                    g = keep.tile([P, width], F32, name="g", bufs=4)
                 nc.vector.tensor_tensor(
                     g[:],
                     y[a][:].indirect(pos_sb[d][:, j0 // 16 : (j0 + width) // 16]),
@@ -133,7 +149,7 @@ def tile_picked_ynca_add_po_kernel(
                 terms.append(g[:])
             for n, term in enumerate(terms):
                 for b, region in enumerate(regions):
-                    nc.tensor.matmul(region, term[:, b * P : (b + 1) * P], ident[:], start=(n == 0), stop=(n == 2), is_transpose=True)
+                    nc.tensor.matmul(region, term[:, b * P : (b + 1) * P], ident[:], start=False, stop=(closes and n == 1), is_transpose=True)
 
         def activate(jb, source, a0, a1):
             nc.scalar.activation(
@@ -178,18 +194,18 @@ def tile_picked_ynca_add_po_kernel(
             nc.vector.quantize_mx(out_codes[:, cols].bitcast(FP8X4), out_scales[:, cols], new_bf[:].rearrange("p c t -> p (c t)"))
             nc.sync.dma_start(out_words[:, cols], out_codes[:, cols].bitcast(I32))
 
-        last = blocks - 1
         for a in range(4):
-            perceive(0, last * P, a, [hT_bank[jb][:, a * P : (a + 1) * P] for jb in range(last)])
-        quantise_w2()
+            perceive(0, last * P, a, [hT_bank[jb][:, a * P : (a + 1) * P] for jb in range(last)], a == 3)
+        w2_codes = quantise_w2()
         for jb in range(last):
             activate(jb, hT_bank[jb][:], 0, 4)
             quantise_h(jb)
         for a in range(3):
-            perceive(last * P, P, a, [hT_bank[last][:, a * P : (a + 1) * P]])
+            perceive(last * P, P, a, [hT_bank[last][:, a * P : (a + 1) * P]], a == 2)
         activate(last, hT_bank[last][:, 0 : 3 * P], 0, 3)
         spare = psum.tile([P, P], F32, name="hT0")
-        perceive(last * P, P, 3, [spare[:]])
+        nc.tensor.matmul(spare[:], y[3][:, last * P : S], ident[:], start=True, stop=False, is_transpose=True)
+        perceive(last * P, P, 3, [spare[:]], True)
         activate(last, spare[:], 3, 4)
         quantise_h(last)
         for jb in range(blocks):

@@ -177,26 +177,36 @@ def tile_picked_ynca_add_po_kernel(
         def update(jb):
             cols = slice(jb * P, (jb + 1) * P)
             h_codes, h_scales = h_mx[jb]
-            rr = psum.tile([P, PACK, P], F32, name="rr", tag="acc", bufs=2)
+            if jb < 2:
+                rr = psum.tile([P, PACK, P], F32, name="rr", tag="acc", bufs=2)
+            else:
+                rr = psum.tile([P, PACK, P], F32, name="hT%d" % (jb - 1))
             for t in range(PACK):
                 m = slice(t * P, (t + 1) * P)
                 nc.tensor.matmul_mx(
                     rr[:, t, :], w2_codes[:, m].bitcast(FP8X4), w2_scales[:, m], h_codes[:].bitcast(FP8X4), h_scales[:], start=True, stop=True
                 )
             new = keep.tile([P, PACK, P], F32, name="new%d" % jb)
+            new_bf = keep.tile([P, P, PACK], BF16, name="new_bf%d" % jb, align_bytes=64)
             nc.vector.tensor_tensor(new[:], rr[:], cur_sb[:, :, cols], ADD)
             nc.sync.dma_start(out_rows[:, :, cols], new[:])
-            new_bf = keep.tile([P, P, PACK], BF16, name="new_bf%d" % jb, align_bytes=64)
-            nc.scalar.copy(
-                new_bf[:].rearrange("p (c i) t -> p c t i", i=4),
-                new[:].rearrange("p t (c i) -> p c t i", i=4),
-            )
+            if jb == last:
+                nc.vector.tensor_tensor(new_bf[:], rr[:].rearrange("p t j -> p j t"), cur_last[:], ADD)
+            if jb < last:
+                nc.scalar.copy(
+                    new_bf[:].rearrange("p (c i) t -> p c t i", i=4),
+                    new[:].rearrange("p t (c i) -> p c t i", i=4),
+                )
             nc.vector.quantize_mx(out_codes[:, cols].bitcast(FP8X4), out_scales[:, cols], new_bf[:].rearrange("p c t -> p (c t)"))
-            nc.sync.dma_start(out_words[:, cols], out_codes[:, cols].bitcast(I32))
+            if jb >= last - 1:
+                done = slice(0, last * P) if jb < last else cols
+                nc.sync.dma_start(out_words[:, done], out_codes[:, done].bitcast(I32))
 
         for a in range(4):
             perceive(0, last * P, a, [hT_bank[jb][:, a * P : (a + 1) * P] for jb in range(last)], a == 3)
         w2_codes = quantise_w2()
+        cur_last = keep.tile([P, P, PACK], F32, name="cur_last")
+        nc.scalar.copy(cur_last[:], cur_sb[:, :, last * P : S].rearrange("p t j -> p j t"))
         for jb in range(last):
             activate(jb, hT_bank[jb][:], 0, 4)
             quantise_h(jb)

@@ -45,7 +45,7 @@ def tile_picked_ynca_add_po_kernel(
 
         w1_rows = w1.rearrange("(p j) c -> p j c", j=PACK)
         w1_raw = []
-        kern_sb = keep.tile([P, 2, S], F32, name="kern_sb")
+        kern_sb = [keep.tile([P, S], F32, name="kern_sb%d" % d) for d in range(2)]
         for n, (c0, width) in enumerate(W1_LOADS):
             raw = keep.tile([P, PACK, width], F32, name="w1_raw%d" % n)
             nc.sync.dma_start(raw[:], w1_rows[:, :, c0 : c0 + width])
@@ -54,9 +54,10 @@ def tile_picked_ynca_add_po_kernel(
             if n == 0:
                 nc.sync.dma_start(xw[:].bitcast(I32), x_words[0].rearrange("p c r -> p (c r)").bitcast(I32))
             if n == 1:
-                nc.sync.dma_start(kern_sb[:], kern.rearrange("d p j -> p d j"))
+                nc.sync.dma_start(kern_sb[0][:], kern[0])
                 nc.sync.dma_start(pos_sb[0][:], pos1)
                 nc.sync.dma_start(pos_sb[1][:], pos2)
+        nc.sync.dma_start(kern_sb[1][:], kern[1])
         w2_raw = keep.tile([P, PACK, N], F32, name="w2_raw")
         nc.sync.dma_start(w2_raw[:], w2.rearrange("(p j) c -> p j c", j=PACK))
         fire_col = keep.tile([P, S // P], F32, name="fire_col")
@@ -108,11 +109,8 @@ def tile_picked_ynca_add_po_kernel(
             nc.scalar.copy(y_a[:], bank[:])
             y.append(y_a)
         hT_bank = [psum.tile([P, H], F32, name="hT%d" % jb) for jb in range(blocks)]
-        for a in range(H // P):
-            for jb in range(blocks if a < 3 else last):
-                nc.tensor.matmul(
-                    hT_bank[jb][:, a * P : (a + 1) * P], y[a][:, jb * P : (jb + 1) * P], ident[:], start=(a == 0), stop=False, is_transpose=True
-                )
+        for a in range(3):
+            nc.tensor.matmul(hT_bank[last][:, a * P : (a + 1) * P], y[a][:, last * P : S], ident[:], start=(a == 0), stop=False, is_transpose=True)
 
         w2_bf = keep.tile([P, PACK, P, PACK], BF16, name="w2_bf", align_bytes=64)
         w2_scales = keep.tile([P, N], U8, name="w2_scales", align_bytes=64)
@@ -143,7 +141,7 @@ def tile_picked_ynca_add_po_kernel(
                 nc.vector.tensor_tensor(
                     g[:],
                     y[a][:].indirect(pos_sb[d][:, j0 // 16 : (j0 + width) // 16]),
-                    kern_sb[:, d, j0 : j0 + width],
+                    kern_sb[d][:, j0 : j0 + width],
                     MULT,
                 )
                 terms.append(g[:])
@@ -203,6 +201,10 @@ def tile_picked_ynca_add_po_kernel(
                 nc.sync.dma_start(out_words[:, done], out_codes[:, done].bitcast(I32))
 
         for a in range(4):
+            for jb in range(last):
+                nc.tensor.matmul(
+                    hT_bank[jb][:, a * P : (a + 1) * P], y[a][:, jb * P : (jb + 1) * P], ident[:], start=(a == 0), stop=False, is_transpose=True
+                )
             perceive(0, last * P, a, [hT_bank[jb][:, a * P : (a + 1) * P] for jb in range(last)], a == 3)
         w2_codes = quantise_w2()
         cur_last = keep.tile([P, P, PACK], F32, name="cur_last")

@@ -19,8 +19,15 @@ RELU = mybir.ActivationFunctionType.Relu
 
 P = 128
 PACK = 4
-CHUNKS = [(0, 384), (384, 128)]
-W1_LOADS = [(0, 128), (128, 128), (256, 256)]
+LIST_ROWS = 16
+QUADRANT = 32
+QUARTERS = H // P
+BLOCKS = S // P
+LAST = BLOCKS - 1
+HALF = S // 2
+W1_LOADS = [(0, P), (P, P), (2 * P, 2 * P)]
+PRODUCT_SLOTS = 4
+WIDE_GATHER_SLOT = {(0, 1): "w1_bf2", (1, 0): "w1_bf3", (3, 0): "w2_codes"}
 
 
 def tile_picked_ynca_add_po_kernel(
@@ -32,15 +39,27 @@ def tile_picked_ynca_add_po_kernel(
         keep = ctx.enter_context(tc.tile_pool(name="keep", bufs=1))
         psum = ctx.enter_context(tc.psum_pool(name="psum", bufs=1))
 
-        offs_sb = lists.tile([P, S // 16], U16, name="offs_sb")
-        pos_sb = [lists.tile([P, S // 16], U16, name="pos_sb%d" % d) for d in range(2)]
+        offs_sb = lists.tile([P, S // LIST_ROWS], U16, name="offs_sb")
+        pos_sb = [lists.tile([P, S // LIST_ROWS], U16, name="pos_sb%d" % d) for d in range(2)]
+
+        def scale_rows(tile, q):
+            return tile[QUADRANT * q : QUADRANT * q + PACK, :].bitcast(I32)
+
+        def round_and_interleave(grouped, planes):
+            nc.scalar.copy(
+                grouped.rearrange("p (c i) t -> p c t i", i=4),
+                planes.rearrange("p t (c i) -> p c t i", i=4),
+            )
+
+        def add_transposed(region, columns, start, stop):
+            nc.tensor.matmul(region, columns, ident[:], start=start, stop=stop, is_transpose=True)
 
         nc.sync.dma_start(offs_sb[:], offs)
         xs = keep.tile([P, T], U8, name="xs", align_bytes=64)
         nc.gpsimd.memset(xs[:].bitcast(I32), 0)
         for q in range(4):
             queue = nc.scalar if q < 2 else nc.sync
-            queue.dma_start(xs[32 * q : 32 * q + 4, :].bitcast(I32), x_scales[0, 4 * q : 4 * q + 4, :].bitcast(I32))
+            queue.dma_start(scale_rows(xs, q), x_scales[0, PACK * q : PACK * (q + 1), :].bitcast(I32))
         xw = keep.tile([P, T], U32, name="xw", align_bytes=64)
 
         w1_rows = w1.rearrange("(p j) c -> p j c", j=PACK)
@@ -60,7 +79,7 @@ def tile_picked_ynca_add_po_kernel(
         nc.sync.dma_start(kern_sb[1][:], kern[1])
         w2_raw = keep.tile([P, PACK, N], F32, name="w2_raw")
         nc.sync.dma_start(w2_raw[:], w2.rearrange("(p j) c -> p j c", j=PACK))
-        fire_col = keep.tile([P, S // P], F32, name="fire_col")
+        fire_col = keep.tile([P, BLOCKS], F32, name="fire_col")
         with nc.allow_non_contiguous_dma(reason="one value a partition"):
             nc.sync.dma_start(fire_col[:], fire[0].rearrange("(b p) -> p b", p=P))
         cur_sb = keep.tile([P, PACK, S], F32, name="cur_sb")
@@ -71,19 +90,12 @@ def tile_picked_ynca_add_po_kernel(
 
         gs = keep.tile([P, S], U8, name="gs", align_bytes=64)
         nc.vector.tensor_copy(gs[:], xs[:].indirect(offs_sb[:]))
-        half = S // 2
         gw = []
-        blocks = S // P
-        last = blocks - 1
-
         y = []
         w1_mx = []
-        for a in range(H // P):
+        for a in range(QUARTERS):
             grouped = keep.tile([P, P, PACK], BF16, name="w1_bf%d" % a, align_bytes=64)
-            nc.scalar.copy(
-                grouped[:].rearrange("p (c i) t -> p c t i", i=4),
-                w1_raw[a].rearrange("p t (c i) -> p c t i", i=4),
-            )
+            round_and_interleave(grouped[:], w1_raw[a])
             codes = keep.tile([P, P], U32, name="w1_codes%d" % a, align_bytes=64)
             scales = keep.tile([P, P], U8, name="w1_scales%d" % a, align_bytes=64)
             nc.vector.quantize_mx(codes[:].bitcast(FP8X4), scales[:], grouped[:].rearrange("p c t -> p (c t)"))
@@ -91,77 +103,69 @@ def tile_picked_ynca_add_po_kernel(
             if a == 0:
                 y_a = keep.tile([P, S], F32, name="y0")
                 for n in range(2):
-                    cols = slice(n * half, (n + 1) * half)
-                    gw.append(keep.tile([P, half], U32, name=("gw0", "w1_bf0")[n], align_bytes=64))
-                    nc.vector.tensor_copy(gw[n][:], xw[:].indirect(offs_sb[:, n * half // 16 : (n + 1) * half // 16]))
-                    bank = psum.tile([P, half], F32, name="ybank", tag="acc", bufs=2)
+                    cols = slice(n * HALF, (n + 1) * HALF)
+                    gw.append(keep.tile([P, HALF], U32, name=("gw0", "w1_bf0")[n], align_bytes=64))
+                    nc.vector.tensor_copy(gw[n][:], xw[:].indirect(offs_sb[:, cols.start // LIST_ROWS : cols.stop // LIST_ROWS]))
+                    bank = psum.tile([P, HALF], F32, name="ybank", tag="acc", bufs=2)
                     nc.tensor.matmul_mx(bank[:], codes[:].bitcast(FP8X4), scales[:], gw[n][:].bitcast(FP8X4), gs[:, cols], start=True, stop=True)
                     copy = nc.vector.tensor_copy if n else nc.scalar.copy
                     copy(y_a[:, cols], bank[:])
                 y.append(y_a)
-        for a in range(1, H // P):
+        for a in range(1, QUARTERS):
             codes, scales = w1_mx[a]
             bank = psum.tile([P, S], F32, name="hT%d" % (a - 1))
             for n in range(2):
-                cols = slice(n * half, (n + 1) * half)
+                cols = slice(n * HALF, (n + 1) * HALF)
                 nc.tensor.matmul_mx(bank[:, cols], codes[:].bitcast(FP8X4), scales[:], gw[n][:].bitcast(FP8X4), gs[:, cols], start=True, stop=True)
             y_a = keep.tile([P, S], F32, name="w1_raw2" if a == 1 else "y%d" % a)
             nc.scalar.copy(y_a[:], bank[:])
             y.append(y_a)
-        hT_bank = [psum.tile([P, H], F32, name="hT%d" % jb) for jb in range(blocks)]
-        for a in range(3):
-            nc.tensor.matmul(hT_bank[last][:, a * P : (a + 1) * P], y[a][:, last * P : S], ident[:], start=(a == 0), stop=False, is_transpose=True)
+
+        hT_bank = [psum.tile([P, H], F32, name="hT%d" % jb) for jb in range(BLOCKS)]
+
+        def region(jb, a):
+            return hT_bank[jb][:, a * P : (a + 1) * P]
+
+        for a in range(QUARTERS - 1):
+            add_transposed(region(LAST, a), y[a][:, LAST * P : S], a == 0, False)
 
         w2_bf = keep.tile([P, PACK, P, PACK], BF16, name="w2_bf", align_bytes=64)
         w2_scales = keep.tile([P, N], U8, name="w2_scales", align_bytes=64)
-
-        def quantise_w2():
-            w2_codes = keep.tile([P, N], U32, name="w2_codes", align_bytes=64)
-            for t in range(PACK):
-                nc.scalar.copy(w2_bf[:, t], w2_raw[:].rearrange("p j (m t) -> p t m j", t=PACK)[:, t])
-            nc.vector.quantize_mx(w2_codes[:].bitcast(FP8X4), w2_scales[:], w2_bf[:].rearrange("p t m j -> p (t m j)"))
-            return w2_codes
-
         out_codes = keep.tile([P, S], U32, name="out_codes", align_bytes=64)
         out_scales = keep.tile([P, S], U8, name="out_scales", align_bytes=64)
         out_rows = out_0.rearrange("(p t) j -> p t j", t=PACK)
         out_words = out_1[0].rearrange("p c r -> p (c r)").bitcast(I32)
+        hT_bf = [keep.tile([P, H], BF16, name="hT_bf%d" % jb) for jb in range(BLOCKS)]
 
-        hT_bf = [keep.tile([P, H], BF16, name="hT_bf%d" % jb) for jb in range(blocks)]
-
-        def perceive(j0, width, a, regions, closes):
+        def perceive(j0, a, regions, closes):
+            width = len(regions) * P
             terms = []
             for d in range(2):
-                if j0 == 0 and 2 * a + d in (1, 2):
-                    g = keep.tile([P, width], F32, name="w1_bf%d" % (2 * a + d + 1), align_bytes=64)
-                elif j0 == 0 and 2 * a + d == 6:
-                    g = keep.tile([P, width], F32, name="w2_codes", align_bytes=64)
+                if j0 == 0 and (a, d) in WIDE_GATHER_SLOT:
+                    g = keep.tile([P, width], F32, name=WIDE_GATHER_SLOT[(a, d)], align_bytes=64)
                 else:
-                    g = keep.tile([P, width], F32, name="g", bufs=4)
+                    g = keep.tile([P, width], F32, name="g", bufs=PRODUCT_SLOTS)
                 nc.vector.tensor_tensor(
                     g[:],
-                    y[a][:].indirect(pos_sb[d][:, j0 // 16 : (j0 + width) // 16]),
+                    y[a][:].indirect(pos_sb[d][:, j0 // LIST_ROWS : (j0 + width) // LIST_ROWS]),
                     kern_sb[d][:, j0 : j0 + width],
                     MULT,
                 )
                 terms.append(g[:])
-            for n, term in enumerate(terms):
-                for b, region in enumerate(regions):
-                    nc.tensor.matmul(region, term[:, b * P : (b + 1) * P], ident[:], start=False, stop=(closes and n == 1), is_transpose=True)
+            for d, term in enumerate(terms):
+                for b, target in enumerate(regions):
+                    add_transposed(target, term[:, b * P : (b + 1) * P], False, closes and d == 1)
 
         def activate(jb, source, a0, a1):
             nc.scalar.activation(
-                hT_bf[jb][:].rearrange("j (u p e) -> j u p e", u=2, e=2)[:, :, 32 * a0 : 32 * a1, :],
+                hT_bf[jb][:].rearrange("j (u p e) -> j u p e", u=2, e=2)[:, :, P // PACK * a0 : P // PACK * a1, :],
                 source.rearrange("j (p u e) -> j u p e", u=2, e=2),
                 RELU,
                 scale=fire_col[:, jb : jb + 1],
             )
 
-        h_mx = dict()
-
         def quantise_h(jb):
-            hT = hT_bf[jb]
-            words = hT[:].bitcast(F32)
+            words = hT_bf[jb][:].bitcast(F32)
             back = psum.tile([P, 2, P], F32, name="back", bufs=2)
             for u in range(2):
                 nc.tensor.transpose(back[:, u, :], words[:, u * P : (u + 1) * P], ident[:])
@@ -170,11 +174,10 @@ def tile_picked_ynca_add_po_kernel(
             h_codes = keep.tile([P, P], U32, name="h_codes%d" % jb, align_bytes=64)
             h_scales = keep.tile([P, P], U8, name="h_scales%d" % jb, align_bytes=64)
             nc.vector.quantize_mx(h_codes[:].bitcast(FP8X4), h_scales[:], h_bf[:])
-            h_mx.setdefault(jb, (h_codes, h_scales))
+            return h_codes, h_scales
 
-        def update(jb):
+        def update(jb, h_codes, h_scales):
             cols = slice(jb * P, (jb + 1) * P)
-            h_codes, h_scales = h_mx[jb]
             if jb < 2:
                 rr = psum.tile([P, PACK, P], F32, name="rr", tag="acc", bufs=2)
             else:
@@ -188,40 +191,46 @@ def tile_picked_ynca_add_po_kernel(
             new_bf = keep.tile([P, P, PACK], BF16, name="new_bf%d" % jb, align_bytes=64)
             nc.vector.tensor_tensor(new[:], rr[:], cur_sb[:, :, cols], ADD)
             nc.sync.dma_start(out_rows[:, :, cols], new[:])
-            if jb == last:
+            if jb == LAST:
                 nc.vector.tensor_tensor(new_bf[:], rr[:].rearrange("p t j -> p j t"), cur_last[:], ADD)
-            if jb < last:
-                nc.scalar.copy(
-                    new_bf[:].rearrange("p (c i) t -> p c t i", i=4),
-                    new[:].rearrange("p t (c i) -> p c t i", i=4),
-                )
+            else:
+                round_and_interleave(new_bf[:], new[:])
             nc.vector.quantize_mx(out_codes[:, cols].bitcast(FP8X4), out_scales[:, cols], new_bf[:].rearrange("p c t -> p (c t)"))
-            if jb >= last - 1:
-                done = slice(0, last * P) if jb < last else cols
+            if jb >= LAST - 1:
+                done = cols if jb == LAST else slice(0, LAST * P)
                 nc.sync.dma_start(out_words[:, done], out_codes[:, done].bitcast(I32))
 
-        for a in range(4):
-            for jb in range(last):
-                nc.tensor.matmul(
-                    hT_bank[jb][:, a * P : (a + 1) * P], y[a][:, jb * P : (jb + 1) * P], ident[:], start=(a == 0), stop=False, is_transpose=True
-                )
-            perceive(0, last * P, a, [hT_bank[jb][:, a * P : (a + 1) * P] for jb in range(last)], a == 3)
-        w2_codes = quantise_w2()
+        for a in range(QUARTERS):
+            for jb in range(LAST):
+                add_transposed(region(jb, a), y[a][:, jb * P : (jb + 1) * P], a == 0, False)
+            perceive(0, a, [region(jb, a) for jb in range(LAST)], a == QUARTERS - 1)
+
+        w2_codes = keep.tile([P, N], U32, name="w2_codes", align_bytes=64)
+        for m0 in range(0, P, P // 4):
+            nc.scalar.copy(
+                w2_bf[:].rearrange("p t m j -> p m t j")[:, m0 : m0 + P // 4],
+                w2_raw[:].rearrange("p j (m t) -> p m t j", t=PACK)[:, m0 : m0 + P // 4],
+            )
+        nc.vector.quantize_mx(w2_codes[:].bitcast(FP8X4), w2_scales[:], w2_bf[:].rearrange("p t m j -> p (t m j)"))
         cur_last = keep.tile([P, P, PACK], F32, name="cur_last")
-        nc.scalar.copy(cur_last[:], cur_sb[:, :, last * P : S].rearrange("p t j -> p j t"))
-        for jb in range(last):
-            activate(jb, hT_bank[jb][:], 0, 4)
-            quantise_h(jb)
-        for a in range(3):
-            perceive(last * P, P, a, [hT_bank[last][:, a * P : (a + 1) * P]], a == 2)
-        activate(last, hT_bank[last][:, 0 : 3 * P], 0, 3)
+        nc.scalar.copy(cur_last[:], cur_sb[:, :, LAST * P : S].rearrange("p t j -> p j t"))
+
+        h_mx = []
+        for jb in range(LAST):
+            activate(jb, hT_bank[jb][:], 0, QUARTERS)
+            h_mx.append(quantise_h(jb))
+
+        for a in range(QUARTERS - 1):
+            perceive(LAST * P, a, [region(LAST, a)], a == QUARTERS - 2)
+        activate(LAST, hT_bank[LAST][:, 0 : (QUARTERS - 1) * P], 0, QUARTERS - 1)
         spare = psum.tile([P, P], F32, name="hT0")
-        nc.tensor.matmul(spare[:], y[3][:, last * P : S], ident[:], start=True, stop=False, is_transpose=True)
-        perceive(last * P, P, 3, [spare[:]], True)
-        activate(last, spare[:], 3, 4)
-        quantise_h(last)
-        for jb in range(blocks):
-            update(jb)
+        add_transposed(spare[:], y[QUARTERS - 1][:, LAST * P : S], True, False)
+        perceive(LAST * P, QUARTERS - 1, [spare[:]], True)
+        activate(LAST, spare[:], QUARTERS - 1, QUARTERS)
+        h_mx.append(quantise_h(LAST))
+
+        for jb in range(BLOCKS):
+            update(jb, *h_mx[jb])
         for q in range(4):
             queue = nc.sync if q % 2 else nc.scalar
-            queue.dma_start(out_2[0, 4 * q : 4 * q + 4, :].bitcast(I32), out_scales[32 * q : 32 * q + 4, :].bitcast(I32))
+            queue.dma_start(out_2[0, PACK * q : PACK * (q + 1), :].bitcast(I32), scale_rows(out_scales, q))

@@ -27,7 +27,7 @@ LAST = BLOCKS - 1
 HALF = S // 2
 W1_LOADS = [(0, P), (P, P), (2 * P, 2 * P)]
 PRODUCT_SLOTS = 4
-WIDE_GATHER_SLOT = {(0, 1): "w1_bf2", (1, 0): "w1_bf3", (3, 0): "w2_codes"}
+WIDE_GATHER_SLOT = {(3, 0): "w2_codes"}
 
 
 def tile_picked_ynca_add_po_kernel(
@@ -37,6 +37,7 @@ def tile_picked_ynca_add_po_kernel(
     with ExitStack() as ctx:
         lists = ctx.enter_context(tc.tile_pool(name="lists", bufs=1))
         keep = ctx.enter_context(tc.tile_pool(name="keep", bufs=1))
+        shared = ctx.enter_context(tc.tile_pool(name="shared", bufs=1))
         psum = ctx.enter_context(tc.psum_pool(name="psum", bufs=1))
 
         offs_sb = lists.tile([P, S // LIST_ROWS], U16, name="offs_sb")
@@ -56,22 +57,26 @@ def tile_picked_ynca_add_po_kernel(
 
         nc.sync.dma_start(offs_sb[:], offs)
         xs = keep.tile([P, T], U8, name="xs", align_bytes=64)
-        nc.gpsimd.memset(xs[:].bitcast(I32), 0)
         for q in range(4):
             queue = nc.scalar if q < 2 else nc.sync
-            queue.dma_start(scale_rows(xs, q), x_scales[0, PACK * q : PACK * (q + 1), :].bitcast(I32))
+            rows = x_scales[0, PACK * q : PACK * (q + 1), :].bitcast(I32)
+            queue.dma_start(
+                xs[QUADRANT * q : QUADRANT * (q + 1), :].bitcast(I32), rows.unsqueeze(0).to_broadcast([QUADRANT // PACK, PACK, T // 4])
+            )
         xw = keep.tile([P, T], U32, name="xw", align_bytes=64)
+        nc.sync.dma_start(xw[:].bitcast(I32), x_words[0].rearrange("p c r -> p (c r)").bitcast(I32))
 
         w1_rows = w1.rearrange("(p j) c -> p j c", j=PACK)
         w1_raw = []
         kern_sb = [keep.tile([P, S], F32, name="kern_sb%d" % d) for d in range(2)]
         for n, (c0, width) in enumerate(W1_LOADS):
-            raw = keep.tile([P, PACK, width], F32, name="w1_raw%d" % n)
+            if n == 2:
+                raw = shared.tile([P, PACK, width], F32, name="w1_raw2", offset=0)
+            else:
+                raw = keep.tile([P, PACK, width], F32, name="w1_raw%d" % n)
             nc.sync.dma_start(raw[:], w1_rows[:, :, c0 : c0 + width])
             for a0 in range(0, width, P):
                 w1_raw.append(raw[:, :, a0 : a0 + P])
-            if n == 0:
-                nc.sync.dma_start(xw[:].bitcast(I32), x_words[0].rearrange("p c r -> p (c r)").bitcast(I32))
             if n == 1:
                 nc.sync.dma_start(kern_sb[0][:], kern[0])
                 nc.sync.dma_start(pos_sb[0][:], pos1)
@@ -90,34 +95,38 @@ def tile_picked_ynca_add_po_kernel(
 
         gs = keep.tile([P, S], U8, name="gs", align_bytes=64)
         nc.vector.tensor_copy(gs[:], xs[:].indirect(offs_sb[:]))
-        gw = []
+        gw = keep.tile([P, S], U32, name="gw", align_bytes=64)
         y = []
         w1_mx = []
-        for a in range(QUARTERS):
-            grouped = keep.tile([P, P, PACK], BF16, name="w1_bf%d" % a, align_bytes=64)
-            round_and_interleave(grouped[:], w1_raw[a])
-            codes = keep.tile([P, P], U32, name="w1_codes%d" % a, align_bytes=64)
-            scales = keep.tile([P, P], U8, name="w1_scales%d" % a, align_bytes=64)
+        for a0, a1 in ((0, 1), (1, 2), (2, 4)):
+            width = (a1 - a0) * P
+            grouped = keep.tile([P, width, PACK], BF16, name="w1_bf%d" % a0, align_bytes=64)
+            for a in range(a0, a1):
+                round_and_interleave(grouped[:, (a - a0) * P : (a - a0 + 1) * P, :], w1_raw[a])
+            codes = keep.tile([P, width], U32, name="w1_codes%d" % a0, align_bytes=64)
+            scales = keep.tile([P, width], U8, name="w1_scales%d" % a0, align_bytes=64)
             nc.vector.quantize_mx(codes[:].bitcast(FP8X4), scales[:], grouped[:].rearrange("p c t -> p (c t)"))
-            w1_mx.append((codes, scales))
-            if a == 0:
+            for a in range(a0, a1):
+                cols = slice((a - a0) * P, (a - a0 + 1) * P)
+                w1_mx.append((codes[:, cols], scales[:, cols]))
+            if a0 == 0:
                 y_a = keep.tile([P, S], F32, name="y0")
                 for n in range(2):
                     cols = slice(n * HALF, (n + 1) * HALF)
-                    gw.append(keep.tile([P, HALF], U32, name=("gw0", "w1_bf0")[n], align_bytes=64))
-                    nc.vector.tensor_copy(gw[n][:], xw[:].indirect(offs_sb[:, cols.start // LIST_ROWS : cols.stop // LIST_ROWS]))
+                    nc.vector.tensor_copy(gw[:, cols], xw[:].indirect(offs_sb[:, cols.start // LIST_ROWS : cols.stop // LIST_ROWS]))
                     bank = psum.tile([P, HALF], F32, name="ybank", tag="acc", bufs=2)
-                    nc.tensor.matmul_mx(bank[:], codes[:].bitcast(FP8X4), scales[:], gw[n][:].bitcast(FP8X4), gs[:, cols], start=True, stop=True)
+                    nc.tensor.matmul_mx(bank[:], codes[:].bitcast(FP8X4), scales[:], gw[:, cols].bitcast(FP8X4), gs[:, cols], start=True, stop=True)
                     copy = nc.vector.tensor_copy if n else nc.scalar.copy
                     copy(y_a[:, cols], bank[:])
                 y.append(y_a)
         for a in range(1, QUARTERS):
             codes, scales = w1_mx[a]
             bank = psum.tile([P, S], F32, name="hT%d" % (a - 1))
-            for n in range(2):
-                cols = slice(n * HALF, (n + 1) * HALF)
-                nc.tensor.matmul_mx(bank[:, cols], codes[:].bitcast(FP8X4), scales[:], gw[n][:].bitcast(FP8X4), gs[:, cols], start=True, stop=True)
-            y_a = keep.tile([P, S], F32, name="w1_raw2" if a == 1 else "y%d" % a)
+            nc.tensor.matmul_mx(bank[:], codes.bitcast(FP8X4), scales, gw[:].bitcast(FP8X4), gs[:], start=True, stop=True)
+            if a == 1:
+                y_a = shared.tile([P, S], F32, name="y1", offset=0)
+            else:
+                y_a = keep.tile([P, S], F32, name="y%d" % a)
             nc.scalar.copy(y_a[:], bank[:])
             y.append(y_a)
 
@@ -141,7 +150,9 @@ def tile_picked_ynca_add_po_kernel(
             width = len(regions) * P
             terms = []
             for d in range(2):
-                if j0 == 0 and (a, d) in WIDE_GATHER_SLOT:
+                if j0 == 0 and (a, d) == (0, 1):
+                    g = shared.tile([P, width], F32, name="g01", offset=2048)
+                elif j0 == 0 and (a, d) in WIDE_GATHER_SLOT:
                     g = keep.tile([P, width], F32, name=WIDE_GATHER_SLOT[(a, d)], align_bytes=64)
                 else:
                     g = keep.tile([P, width], F32, name="g", bufs=PRODUCT_SLOTS)
@@ -189,11 +200,16 @@ def tile_picked_ynca_add_po_kernel(
                 )
             new = keep.tile([P, PACK, P], F32, name="new%d" % jb)
             new_bf = keep.tile([P, P, PACK], BF16, name="new_bf%d" % jb, align_bytes=64)
-            nc.vector.tensor_tensor(new[:], rr[:], cur_sb[:, :, cols], ADD)
-            nc.sync.dma_start(out_rows[:, :, cols], new[:])
             if jb == LAST:
-                nc.vector.tensor_tensor(new_bf[:], rr[:].rearrange("p t j -> p j t"), cur_last[:], ADD)
+                for n in range(2):
+                    part = slice(n * P // 2, (n + 1) * P // 2)
+                    nc.vector.tensor_tensor(new[:, :, part], rr[:, :, part], cur_sb[:, :, cols][:, :, part], ADD)
+                nc.sync.dma_start(out_rows[:, :, cols], new[:])
+                round_and_interleave(new_bf[:, 0 : P // 2, :], new[:, :, 0 : P // 2])
+                nc.vector.tensor_tensor(new_bf[:, P // 2 : P, :], rr[:, :, P // 2 : P].rearrange("p t j -> p j t"), cur_last[:], ADD)
             else:
+                nc.vector.tensor_tensor(new[:], rr[:], cur_sb[:, :, cols], ADD)
+                nc.sync.dma_start(out_rows[:, :, cols], new[:])
                 round_and_interleave(new_bf[:], new[:])
             nc.vector.quantize_mx(out_codes[:, cols].bitcast(FP8X4), out_scales[:, cols], new_bf[:].rearrange("p c t -> p (c t)"))
             if jb >= LAST - 1:
@@ -212,8 +228,9 @@ def tile_picked_ynca_add_po_kernel(
                 w2_raw[:].rearrange("p j (m t) -> p m t j", t=PACK)[:, m0 : m0 + P // 4],
             )
         nc.vector.quantize_mx(w2_codes[:].bitcast(FP8X4), w2_scales[:], w2_bf[:].rearrange("p t m j -> p (t m j)"))
-        cur_last = keep.tile([P, P, PACK], F32, name="cur_last")
-        nc.scalar.copy(cur_last[:], cur_sb[:, :, LAST * P : S].rearrange("p t j -> p j t"))
+
+        cur_last = keep.tile([P, P // 2, PACK], F32, name="cur_last")
+        nc.scalar.copy(cur_last[:], cur_sb[:, :, S - P // 2 : S].rearrange("p t j -> p j t"))
 
         h_mx = []
         for jb in range(LAST):

@@ -25,9 +25,9 @@ QUARTERS = H // P
 BLOCKS = S // P
 LAST = BLOCKS - 1
 HALF = S // 2
-W1_LOADS = [(0, P), (P, P), (2 * P, 2 * P)]
+W1_LOADS = [(0, P), (P, 2 * P), (3 * P, P)]
 PRODUCT_SLOTS = 4
-WIDE_GATHER_SLOT = {(3, 0): "w2_codes"}
+SLOT_AT = [8192 + n * 1536 for n in range(4)]
 
 
 def tile_picked_ynca_add_po_kernel(
@@ -70,8 +70,8 @@ def tile_picked_ynca_add_po_kernel(
         w1_raw = []
         kern_sb = [keep.tile([P, S], F32, name="kern_sb%d" % d) for d in range(2)]
         for n, (c0, width) in enumerate(W1_LOADS):
-            if n == 2:
-                raw = shared.tile([P, PACK, width], F32, name="w1_raw2", offset=0)
+            if n:
+                raw = shared.tile([P, PACK, width], F32, name="w1_raw%d" % n, offset=(0, 0, 6144)[n])
             else:
                 raw = keep.tile([P, PACK, width], F32, name="w1_raw%d" % n)
             nc.sync.dma_start(raw[:], w1_rows[:, :, c0 : c0 + width])
@@ -98,7 +98,7 @@ def tile_picked_ynca_add_po_kernel(
         gw = keep.tile([P, S], U32, name="gw", align_bytes=64)
         y = []
         w1_mx = []
-        for a0, a1 in ((0, 1), (1, 2), (2, 4)):
+        for a0, a1 in ((0, 1), (1, 2), (2, 3), (3, 4)):
             width = (a1 - a0) * P
             grouped = keep.tile([P, width, PACK], BF16, name="w1_bf%d" % a0, align_bytes=64)
             for a in range(a0, a1):
@@ -123,8 +123,8 @@ def tile_picked_ynca_add_po_kernel(
             codes, scales = w1_mx[a]
             bank = psum.tile([P, S], F32, name="hT%d" % (a - 1))
             nc.tensor.matmul_mx(bank[:], codes.bitcast(FP8X4), scales, gw[:].bitcast(FP8X4), gs[:], start=True, stop=True)
-            if a == 1:
-                y_a = shared.tile([P, S], F32, name="y1", offset=0)
+            if a < 3:
+                y_a = shared.tile([P, S], F32, name="y%d" % a, offset=(0, 0, 4096 + 32)[a])
             else:
                 y_a = keep.tile([P, S], F32, name="y%d" % a)
             nc.scalar.copy(y_a[:], bank[:])
@@ -150,10 +150,11 @@ def tile_picked_ynca_add_po_kernel(
             width = len(regions) * P
             terms = []
             for d in range(2):
-                if j0 == 0 and (a, d) == (0, 1):
-                    g = shared.tile([P, width], F32, name="g01", offset=2048)
-                elif j0 == 0 and (a, d) in WIDE_GATHER_SLOT:
-                    g = keep.tile([P, width], F32, name=WIDE_GATHER_SLOT[(a, d)], align_bytes=64)
+                if j0 == 0 and (a, d) in ((0, 1), (1, 0)):
+                    g = shared.tile([P, width], F32, name="g%d%d" % (a, d), offset=(2048, 6144 + 64)[a])
+                elif j0 or a >= 2:
+                    at = SLOT_AT[(2 * a + d) % 4]
+                    g = shared.tile([P, width], F32, name="g%d_%d%d" % (j0, a, d), offset=at)
                 else:
                     g = keep.tile([P, width], F32, name="g", bufs=PRODUCT_SLOTS)
                 nc.vector.tensor_tensor(
@@ -175,13 +176,16 @@ def tile_picked_ynca_add_po_kernel(
                 scale=fire_col[:, jb : jb + 1],
             )
 
-        def quantise_h(jb):
+        def turn_back(jb):
             words = hT_bf[jb][:].bitcast(F32)
             back = psum.tile([P, 2, P], F32, name="back", bufs=2)
             for u in range(2):
                 nc.tensor.transpose(back[:, u, :], words[:, u * P : (u + 1) * P], ident[:])
             h_bf = keep.tile([P, P * PACK], BF16, name="h_bf%d" % jb, align_bytes=64)
             nc.scalar.copy(h_bf[:].bitcast(F32).rearrange("p (j u) -> p j u", u=2), back[:].rearrange("p u j -> p j u"))
+            return h_bf
+
+        def quantise_h(jb, h_bf):
             h_codes = keep.tile([P, P], U32, name="h_codes%d" % jb, align_bytes=64)
             h_scales = keep.tile([P, P], U8, name="h_scales%d" % jb, align_bytes=64)
             nc.vector.quantize_mx(h_codes[:].bitcast(FP8X4), h_scales[:], h_bf[:])
@@ -212,8 +216,8 @@ def tile_picked_ynca_add_po_kernel(
                 nc.sync.dma_start(out_rows[:, :, cols], new[:])
                 round_and_interleave(new_bf[:], new[:])
             nc.vector.quantize_mx(out_codes[:, cols].bitcast(FP8X4), out_scales[:, cols], new_bf[:].rearrange("p c t -> p (c t)"))
-            if jb >= LAST - 1:
-                done = cols if jb == LAST else slice(0, LAST * P)
+            if jb % 2:
+                done = slice((jb - 1) * P, (jb + 1) * P)
                 nc.sync.dma_start(out_words[:, done], out_codes[:, done].bitcast(I32))
 
         for a in range(QUARTERS):
@@ -221,13 +225,11 @@ def tile_picked_ynca_add_po_kernel(
                 add_transposed(region(jb, a), y[a][:, jb * P : (jb + 1) * P], a == 0, False)
             perceive(0, a, [region(jb, a) for jb in range(LAST)], a == QUARTERS - 1)
 
-        w2_codes = keep.tile([P, N], U32, name="w2_codes", align_bytes=64)
         for m0 in range(0, P, P // 4):
             nc.scalar.copy(
                 w2_bf[:].rearrange("p t m j -> p m t j")[:, m0 : m0 + P // 4],
                 w2_raw[:].rearrange("p j (m t) -> p m t j", t=PACK)[:, m0 : m0 + P // 4],
             )
-        nc.vector.quantize_mx(w2_codes[:].bitcast(FP8X4), w2_scales[:], w2_bf[:].rearrange("p t m j -> p (t m j)"))
 
         cur_last = keep.tile([P, P // 2, PACK], F32, name="cur_last")
         nc.scalar.copy(cur_last[:], cur_sb[:, :, S - P // 2 : S].rearrange("p t j -> p j t"))
@@ -235,7 +237,7 @@ def tile_picked_ynca_add_po_kernel(
         h_mx = []
         for jb in range(LAST):
             activate(jb, hT_bank[jb][:], 0, QUARTERS)
-            h_mx.append(quantise_h(jb))
+            h_mx.append(turn_back(jb))
 
         for a in range(QUARTERS - 1):
             perceive(LAST * P, a, [region(LAST, a)], a == QUARTERS - 2)
@@ -244,7 +246,10 @@ def tile_picked_ynca_add_po_kernel(
         add_transposed(spare[:], y[QUARTERS - 1][:, LAST * P : S], True, False)
         perceive(LAST * P, QUARTERS - 1, [spare[:]], True)
         activate(LAST, spare[:], QUARTERS - 1, QUARTERS)
-        h_mx.append(quantise_h(LAST))
+        h_mx.append(turn_back(LAST))
+        w2_codes = shared.tile([P, N], U32, name="w2_codes", align_bytes=64, offset=SLOT_AT[0] - 2048 + 64)
+        nc.vector.quantize_mx(w2_codes[:].bitcast(FP8X4), w2_scales[:], w2_bf[:].rearrange("p t m j -> p (t m j)"))
+        h_mx = [quantise_h(jb, h_mx[jb]) for jb in range(BLOCKS)]
 
         for jb in range(BLOCKS):
             update(jb, *h_mx[jb])

@@ -16,6 +16,7 @@ FP8X4 = mybir.dt.float8_e4m3fn_x4
 MULT = mybir.AluOpType.mult
 ADD = mybir.AluOpType.add
 RELU = mybir.ActivationFunctionType.Relu
+COPY = mybir.ActivationFunctionType.Copy
 
 P = 128
 PACK = 4
@@ -27,7 +28,8 @@ LAST = BLOCKS - 1
 HALF = S // 2
 W1_LOADS = [(0, P), (P, 2 * P), (3 * P, P)]
 PRODUCT_SLOTS = 4
-SLOT_AT = [8192 + n * 1536 for n in range(4)]
+ON_SCALAR = ((1, 1), (2, 1))
+SLOT_AT = [8192 + n * 1600 for n in range(4)]
 
 
 def tile_picked_ynca_add_po_kernel(
@@ -46,8 +48,8 @@ def tile_picked_ynca_add_po_kernel(
         def scale_rows(tile, q):
             return tile[QUADRANT * q : QUADRANT * q + PACK, :].bitcast(I32)
 
-        def round_and_interleave(grouped, planes):
-            nc.scalar.copy(
+        def round_and_interleave(grouped, planes, copy=nc.scalar.copy):
+            copy(
                 grouped.rearrange("p (c i) t -> p c t i", i=4),
                 planes.rearrange("p t (c i) -> p c t i", i=4),
             )
@@ -71,7 +73,7 @@ def tile_picked_ynca_add_po_kernel(
         kern_sb = [keep.tile([P, S], F32, name="kern_sb%d" % d) for d in range(2)]
         for n, (c0, width) in enumerate(W1_LOADS):
             if n:
-                raw = shared.tile([P, PACK, width], F32, name="w1_raw%d" % n, offset=(0, 0, 6144)[n])
+                raw = shared.tile([P, PACK, width], F32, name="w1_raw%d" % n, offset=(0, 0, 4096)[n])
             else:
                 raw = keep.tile([P, PACK, width], F32, name="w1_raw%d" % n)
             nc.sync.dma_start(raw[:], w1_rows[:, :, c0 : c0 + width])
@@ -82,11 +84,18 @@ def tile_picked_ynca_add_po_kernel(
                 nc.sync.dma_start(pos_sb[0][:], pos1)
                 nc.sync.dma_start(pos_sb[1][:], pos2)
         nc.sync.dma_start(kern_sb[1][:], kern[1])
-        w2_raw = keep.tile([P, PACK, N], F32, name="w2_raw")
+        w2_raw = shared.tile([P, PACK, N], F32, name="w2_raw", offset=16384)
         nc.sync.dma_start(w2_raw[:], w2.rearrange("(p j) c -> p j c", j=PACK))
-        fire_col = keep.tile([P, BLOCKS], F32, name="fire_col")
+        fire_rows = fire[0].rearrange("(b p) -> p b", p=P)
+        fire_of = []
         with nc.allow_non_contiguous_dma(reason="one value a partition"):
-            nc.sync.dma_start(fire_col[:], fire[0].rearrange("(b p) -> p b", p=P))
+            for b0, b1 in ((0, 1), (1, 2), (2, 4)):
+                if b0 < 2:
+                    column = shared.tile([P, 1], F32, name="fire%d" % b0, offset=SLOT_AT[2 * b0] - 32)
+                else:
+                    column = keep.tile([P, 2], F32, name="fire%d" % b0)
+                nc.sync.dma_start(column[:], fire_rows[:, b0:b1])
+                fire_of.extend(column[:, b : b + 1] for b in range(b1 - b0))
         cur_sb = keep.tile([P, PACK, S], F32, name="cur_sb")
         nc.sync.dma_start(cur_sb[:], cur.rearrange("(p t) j -> p t j", t=PACK))
 
@@ -100,10 +109,16 @@ def tile_picked_ynca_add_po_kernel(
         w1_mx = []
         for a0, a1 in ((0, 1), (1, 2), (2, 3), (3, 4)):
             width = (a1 - a0) * P
-            grouped = keep.tile([P, width, PACK], BF16, name="w1_bf%d" % a0, align_bytes=64)
+            if a0 == 1:
+                grouped = shared.tile([P, width, PACK], BF16, name="w1_bf%d" % a0, align_bytes=64, offset=24576)
+            else:
+                grouped = keep.tile([P, width, PACK], BF16, name="w1_bf%d" % a0, align_bytes=64)
             for a in range(a0, a1):
                 round_and_interleave(grouped[:, (a - a0) * P : (a - a0 + 1) * P, :], w1_raw[a])
-            codes = keep.tile([P, width], U32, name="w1_codes%d" % a0, align_bytes=64)
+            if a0 == 3:
+                codes = shared.tile([P, width], U32, name="w1_codes%d" % a0, align_bytes=64, offset=28672)
+            else:
+                codes = keep.tile([P, width], U32, name="w1_codes%d" % a0, align_bytes=64)
             scales = keep.tile([P, width], U8, name="w1_scales%d" % a0, align_bytes=64)
             nc.vector.quantize_mx(codes[:].bitcast(FP8X4), scales[:], grouped[:].rearrange("p c t -> p (c t)"))
             for a in range(a0, a1):
@@ -119,16 +134,28 @@ def tile_picked_ynca_add_po_kernel(
                     copy = nc.vector.tensor_copy if n else nc.scalar.copy
                     copy(y_a[:, cols], bank[:])
                 y.append(y_a)
+        on_scalar = {}
+
+        def fetch_on_scalar(a):
+            if (a, 1) in ON_SCALAR:
+                if a > 1:
+                    g = shared.tile([P, LAST * P], F32, name="fetched%d" % a, offset=SLOT_AT[(2 * a + 1) % 4])
+                else:
+                    g = keep.tile([P, LAST * P], F32, name="fetched%d" % a)
+                nc.scalar.activation(g[:], y[a][:].indirect(pos_sb[1][:, 0 : LAST * P // LIST_ROWS]), COPY)
+                on_scalar[a] = g
+
         for a in range(1, QUARTERS):
             codes, scales = w1_mx[a]
-            bank = psum.tile([P, S], F32, name="hT%d" % (a - 1))
+            bank = psum.tile([P, S], F32, name="ybank", tag="back" if a < 3 else "acc", bufs=2)
             nc.tensor.matmul_mx(bank[:], codes.bitcast(FP8X4), scales, gw[:].bitcast(FP8X4), gs[:], start=True, stop=True)
             if a < 3:
-                y_a = shared.tile([P, S], F32, name="y%d" % a, offset=(0, 0, 4096 + 32)[a])
+                y_a = shared.tile([P, S], F32, name="y%d" % a, offset=(0, 2112, 6080)[a])
             else:
                 y_a = keep.tile([P, S], F32, name="y%d" % a)
             nc.scalar.copy(y_a[:], bank[:])
             y.append(y_a)
+            fetch_on_scalar(a)
 
         hT_bank = [psum.tile([P, H], F32, name="hT%d" % jb) for jb in range(BLOCKS)]
 
@@ -138,51 +165,53 @@ def tile_picked_ynca_add_po_kernel(
         for a in range(QUARTERS - 1):
             add_transposed(region(LAST, a), y[a][:, LAST * P : S], a == 0, False)
 
-        w2_bf = keep.tile([P, PACK, P, PACK], BF16, name="w2_bf", align_bytes=64)
-        w2_scales = keep.tile([P, N], U8, name="w2_scales", align_bytes=64)
+        w2_bf = shared.tile([P, PACK, P, PACK], BF16, name="w2_bf", align_bytes=64, offset=28672)
         out_codes = keep.tile([P, S], U32, name="out_codes", align_bytes=64)
         out_scales = keep.tile([P, S], U8, name="out_scales", align_bytes=64)
         out_rows = out_0.rearrange("(p t) j -> p t j", t=PACK)
         out_words = out_1[0].rearrange("p c r -> p (c r)").bitcast(I32)
-        hT_bf = [keep.tile([P, H], BF16, name="hT_bf%d" % jb) for jb in range(BLOCKS)]
+        hT_bf = [shared.tile([P, H], BF16, name="hT_bf%d" % jb, offset=16384 + 1024 * jb) for jb in range(BLOCKS)]
 
         def perceive(j0, a, regions, closes):
             width = len(regions) * P
             terms = []
             for d in range(2):
-                if j0 == 0 and (a, d) in ((0, 1), (1, 0)):
-                    g = shared.tile([P, width], F32, name="g%d%d" % (a, d), offset=(2048, 6144 + 64)[a])
+                if j0 == 0 and (a, d) in ON_SCALAR:
+                    g = on_scalar[a]
+                elif j0 == 0 and a == 0:
+                    g = shared.tile([P, width], F32, name="g%d%d" % (a, d), offset=(24576, 4160)[d])
                 elif j0 or a >= 2:
-                    at = SLOT_AT[(2 * a + d) % 4]
+                    at = SLOT_AT[(2 * a + d) % 4] - (32 if j0 and a >= 2 and d == 0 else 0)
                     g = shared.tile([P, width], F32, name="g%d_%d%d" % (j0, a, d), offset=at)
                 else:
                     g = keep.tile([P, width], F32, name="g", bufs=PRODUCT_SLOTS)
-                nc.vector.tensor_tensor(
-                    g[:],
-                    y[a][:].indirect(pos_sb[d][:, j0 // LIST_ROWS : (j0 + width) // LIST_ROWS]),
-                    kern_sb[d][:, j0 : j0 + width],
-                    MULT,
-                )
+                fetched = y[a][:].indirect(pos_sb[d][:, j0 // LIST_ROWS : (j0 + width) // LIST_ROWS])
+                if j0 == 0 and (a, d) in ON_SCALAR:
+                    nc.vector.tensor_tensor(g[:], g[:], kern_sb[d][:, 0:width], MULT)
+                else:
+                    nc.vector.tensor_tensor(g[:], fetched, kern_sb[d][:, j0 : j0 + width], MULT)
                 terms.append(g[:])
             for d, term in enumerate(terms):
                 for b, target in enumerate(regions):
                     add_transposed(target, term[:, b * P : (b + 1) * P], False, closes and d == 1)
+
 
         def activate(jb, source, a0, a1):
             nc.scalar.activation(
                 hT_bf[jb][:].rearrange("j (u p e) -> j u p e", u=2, e=2)[:, :, P // PACK * a0 : P // PACK * a1, :],
                 source.rearrange("j (p u e) -> j u p e", u=2, e=2),
                 RELU,
-                scale=fire_col[:, jb : jb + 1],
+                scale=fire_of[jb],
             )
 
         def turn_back(jb):
             words = hT_bf[jb][:].bitcast(F32)
-            back = psum.tile([P, 2, P], F32, name="back", bufs=2)
+            back = psum.tile([P, 2, P], F32, name="back", tag="back", bufs=2)
             for u in range(2):
                 nc.tensor.transpose(back[:, u, :], words[:, u * P : (u + 1) * P], ident[:])
             h_bf = keep.tile([P, P * PACK], BF16, name="h_bf%d" % jb, align_bytes=64)
-            nc.scalar.copy(h_bf[:].bitcast(F32).rearrange("p (j u) -> p j u", u=2), back[:].rearrange("p u j -> p j u"))
+            copy = nc.vector.tensor_copy if jb in (1, 2) else nc.scalar.copy
+            copy(h_bf[:].bitcast(F32).rearrange("p (j u) -> p j u", u=2), back[:].rearrange("p u j -> p j u"))
             return h_bf
 
         def quantise_h(jb, h_bf):
@@ -193,14 +222,17 @@ def tile_picked_ynca_add_po_kernel(
 
         def update(jb, h_codes, h_scales):
             cols = slice(jb * P, (jb + 1) * P)
-            if jb < 2:
-                rr = psum.tile([P, PACK, P], F32, name="rr", tag="acc", bufs=2)
+            if jb == 0:
+                banks = [psum.tile([P, 2, P], F32, name="rr", tag="acc", bufs=2) for n in range(2)]
+                planes = [banks[t // 2][:, t % 2, :] for t in range(PACK)]
             else:
                 rr = psum.tile([P, PACK, P], F32, name="hT%d" % (jb - 1))
+                planes = [rr[:, t, :] for t in range(PACK)]
             for t in range(PACK):
-                m = slice(t * P, (t + 1) * P)
+                m = slice(t % 2 * P, (t % 2 + 1) * P)
+                codes, scales = w2_mx[t // 2]
                 nc.tensor.matmul_mx(
-                    rr[:, t, :], w2_codes[:, m].bitcast(FP8X4), w2_scales[:, m], h_codes[:].bitcast(FP8X4), h_scales[:], start=True, stop=True
+                    planes[t], codes[:, m].bitcast(FP8X4), scales[:, m], h_codes[:].bitcast(FP8X4), h_scales[:], start=True, stop=True
                 )
             new = keep.tile([P, PACK, P], F32, name="new%d" % jb)
             new_bf = keep.tile([P, P, PACK], BF16, name="new_bf%d" % jb, align_bytes=64)
@@ -210,7 +242,18 @@ def tile_picked_ynca_add_po_kernel(
                     nc.vector.tensor_tensor(new[:, :, part], rr[:, :, part], cur_sb[:, :, cols][:, :, part], ADD)
                 nc.sync.dma_start(out_rows[:, :, cols], new[:])
                 round_and_interleave(new_bf[:, 0 : P // 2, :], new[:, :, 0 : P // 2])
-                nc.vector.tensor_tensor(new_bf[:, P // 2 : P, :], rr[:, :, P // 2 : P].rearrange("p t j -> p j t"), cur_last[:], ADD)
+                nc.vector.tensor_tensor(
+                    new_bf[:, P // 2 : P, :].rearrange("p (c i) t -> p c t i", i=4),
+                    rr[:, :, P // 2 : P].rearrange("p t (c i) -> p c t i", i=4),
+                    cur_sb[:, :, S - P // 2 : S].rearrange("p t (c i) -> p c t i", i=4),
+                    ADD,
+                )
+            elif jb == 0:
+                for n in range(2):
+                    pair = slice(2 * n, 2 * n + 2)
+                    nc.vector.tensor_tensor(new[:, pair, :], banks[n][:], cur_sb[:, pair, cols], ADD)
+                    nc.sync.dma_start(out_rows[:, pair, cols], new[:, pair, :])
+                round_and_interleave(new_bf[:], new[:])
             else:
                 nc.vector.tensor_tensor(new[:], rr[:], cur_sb[:, :, cols], ADD)
                 nc.sync.dma_start(out_rows[:, :, cols], new[:])
@@ -227,12 +270,10 @@ def tile_picked_ynca_add_po_kernel(
 
         for m0 in range(0, P, P // 4):
             nc.scalar.copy(
-                w2_bf[:].rearrange("p t m j -> p m t j")[:, m0 : m0 + P // 4],
-                w2_raw[:].rearrange("p j (m t) -> p m t j", t=PACK)[:, m0 : m0 + P // 4],
+                w2_bf[:].rearrange("p t m j -> p m j t")[:, m0 : m0 + P // 4],
+                w2_raw[:].rearrange("p j (m t) -> p m j t", t=PACK)[:, m0 : m0 + P // 4],
             )
 
-        cur_last = keep.tile([P, P // 2, PACK], F32, name="cur_last")
-        nc.scalar.copy(cur_last[:], cur_sb[:, :, S - P // 2 : S].rearrange("p t j -> p j t"))
 
         h_mx = []
         for jb in range(LAST):
@@ -247,9 +288,16 @@ def tile_picked_ynca_add_po_kernel(
         perceive(LAST * P, QUARTERS - 1, [spare[:]], True)
         activate(LAST, spare[:], QUARTERS - 1, QUARTERS)
         h_mx.append(turn_back(LAST))
-        w2_codes = shared.tile([P, N], U32, name="w2_codes", align_bytes=64, offset=SLOT_AT[0] - 2048 + 64)
-        nc.vector.quantize_mx(w2_codes[:].bitcast(FP8X4), w2_scales[:], w2_bf[:].rearrange("p t m j -> p (t m j)"))
-        h_mx = [quantise_h(jb, h_mx[jb]) for jb in range(BLOCKS)]
+        w2_mx = []
+        h_bf = h_mx
+        h_mx = []
+        for jb in range(BLOCKS):
+            if jb < 2:
+                codes = shared.tile([P, N // 2], U32, name="w2_codes%d" % jb, align_bytes=64, offset=(SLOT_AT[0] - 1024 + 64, SLOT_AT[2] - 64)[jb])
+                scales = keep.tile([P, N // 2], U8, name="w2_scales%d" % jb, align_bytes=64)
+                nc.vector.quantize_mx(codes[:].bitcast(FP8X4), scales[:], w2_bf[:, 2 * jb : 2 * jb + 2].rearrange("p t m j -> p (t m j)"))
+                w2_mx.append((codes, scales))
+            h_mx.append(quantise_h(jb, h_bf[jb]))
 
         for jb in range(BLOCKS):
             update(jb, *h_mx[jb])

@@ -26,7 +26,7 @@ QUARTERS = H // P
 BLOCKS = S // P
 LAST = BLOCKS - 1
 HALF = S // 2
-W1_LOADS = [(0, P), (P, 2 * P), (3 * P, P)]
+W1_LOADS = [(0, P), (P, P), (2 * P, P), (3 * P, P)]
 PRODUCT_SLOTS = 4
 ON_SCALAR = ((1, 1), (2, 1))
 SLOT_AT = [8192 + n * 1600 for n in range(4)]
@@ -73,13 +73,13 @@ def tile_picked_ynca_add_po_kernel(
         kern_sb = [keep.tile([P, S], F32, name="kern_sb%d" % d) for d in range(2)]
         for n, (c0, width) in enumerate(W1_LOADS):
             if n:
-                raw = shared.tile([P, PACK, width], F32, name="w1_raw%d" % n, offset=(0, 0, 4096)[n])
+                raw = shared.tile([P, PACK, width], F32, name="w1_raw%d" % n, offset=(0, 0, 2048, 4096)[n])
             else:
                 raw = keep.tile([P, PACK, width], F32, name="w1_raw%d" % n)
             nc.sync.dma_start(raw[:], w1_rows[:, :, c0 : c0 + width])
             for a0 in range(0, width, P):
                 w1_raw.append(raw[:, :, a0 : a0 + P])
-            if n == 1:
+            if n == 2:
                 nc.sync.dma_start(kern_sb[0][:], kern[0])
                 nc.sync.dma_start(pos_sb[0][:], pos1)
                 nc.sync.dma_start(pos_sb[1][:], pos2)
@@ -131,7 +131,7 @@ def tile_picked_ynca_add_po_kernel(
                     nc.vector.tensor_copy(gw[:, cols], xw[:].indirect(offs_sb[:, cols.start // LIST_ROWS : cols.stop // LIST_ROWS]))
                     bank = psum.tile([P, HALF], F32, name="ybank", tag="acc", bufs=2)
                     nc.tensor.matmul_mx(bank[:], codes[:].bitcast(FP8X4), scales[:], gw[:, cols].bitcast(FP8X4), gs[:, cols], start=True, stop=True)
-                    copy = nc.vector.tensor_copy if n else nc.scalar.copy
+                    copy = nc.scalar.copy if n else nc.vector.tensor_copy
                     copy(y_a[:, cols], bank[:])
                 y.append(y_a)
         on_scalar = {}

from contextlib import ExitStack

import concourse.mybir as mybir
from concourse.masks import make_identity

K, T, S, H, N = 512, 1024, 512, 512, 512
FLOPS = 2 * K * H * S + 2 * H * N * S

F32 = mybir.dt.float32
BF16 = mybir.dt.bfloat16
I32 = mybir.dt.int32
U32 = mybir.dt.uint32
U16 = mybir.dt.uint16
U8 = mybir.dt.uint8
FP8X4 = mybir.dt.float8_e4m3fn_x4
MULT = mybir.AluOpType.mult
ADD = mybir.AluOpType.add
RELU = mybir.ActivationFunctionType.Relu
COPY = mybir.ActivationFunctionType.Copy

P = 128
PACK = 4
LIST_ROWS = 16
QUADRANT = 32
QUARTERS = H // P
BLOCKS = S // P
LAST = BLOCKS - 1
HALF = S // 2
W1_LOADS = [(0, P), (P, P), (2 * P, P), (3 * P, P)]
PRODUCT_SLOTS = 4
ON_SCALAR = ((1, 1), (2, 1))
SLOT_AT = [8192 + n * 1600 for n in range(4)]


def tile_picked_ynca_add_po_kernel(
    tc, x_words, x_scales, w1, w2, kern, cur, fire, offs, pos1, pos2, out_0, out_1, out_2
):
    nc = tc.nc
    with ExitStack() as ctx:
        lists = ctx.enter_context(tc.tile_pool(name="lists", bufs=1))
        keep = ctx.enter_context(tc.tile_pool(name="keep", bufs=1))
        shared = ctx.enter_context(tc.tile_pool(name="shared", bufs=1))
        psum = ctx.enter_context(tc.psum_pool(name="psum", bufs=1))

        offs_sb = lists.tile([P, S // LIST_ROWS], U16, name="offs_sb")
        pos_sb = [lists.tile([P, S // LIST_ROWS], U16, name="pos_sb%d" % d) for d in range(2)]

        def scale_rows(tile, q):
            return tile[QUADRANT * q : QUADRANT * q + PACK, :].bitcast(I32)

        def round_and_interleave(grouped, planes, copy=nc.scalar.copy):
            copy(
                grouped.rearrange("p (c i) t -> p c t i", i=4),
                planes.rearrange("p t (c i) -> p c t i", i=4),
            )

        def add_transposed(region, columns, start, stop):
            nc.tensor.matmul(region, columns, ident[:], start=start, stop=stop, is_transpose=True)

        nc.sync.dma_start(offs_sb[:], offs)
        xs = keep.tile([P, T], U8, name="xs", align_bytes=64)
        for q in range(4):
            queue = nc.scalar if q < 2 else nc.sync
            rows = x_scales[0, PACK * q : PACK * (q + 1), :].bitcast(I32)
            queue.dma_start(
                xs[QUADRANT * q : QUADRANT * (q + 1), :].bitcast(I32), rows.unsqueeze(0).to_broadcast([QUADRANT // PACK, PACK, T // 4])
            )
        xw = keep.tile([P, T], U32, name="xw", align_bytes=64)
        nc.sync.dma_start(xw[:].bitcast(I32), x_words[0].rearrange("p c r -> p (c r)").bitcast(I32))

        w1_rows = w1.rearrange("(p j) c -> p j c", j=PACK)
        w1_raw = []
        kern_sb = [keep.tile([P, S], F32, name="kern_sb%d" % d) for d in range(2)]
        for n, (c0, width) in enumerate(W1_LOADS):
            if n:
                raw = shared.tile([P, PACK, width], F32, name="w1_raw%d" % n, offset=(0, 0, 2048, 4096)[n])
            else:
                raw = keep.tile([P, PACK, width], F32, name="w1_raw%d" % n)
            nc.sync.dma_start(raw[:], w1_rows[:, :, c0 : c0 + width])
            for a0 in range(0, width, P):
                w1_raw.append(raw[:, :, a0 : a0 + P])
            if n == 2:
                nc.sync.dma_start(kern_sb[0][:], kern[0])
                nc.sync.dma_start(pos_sb[0][:], pos1)
                nc.sync.dma_start(pos_sb[1][:], pos2)
        nc.sync.dma_start(kern_sb[1][:], kern[1])
        w2_raw = shared.tile([P, PACK, N], F32, name="w2_raw", offset=16384)
        nc.sync.dma_start(w2_raw[:], w2.rearrange("(p j) c -> p j c", j=PACK))
        fire_rows = fire[0].rearrange("(b p) -> p b", p=P)
        fire_of = []
        with nc.allow_non_contiguous_dma(reason="one value a partition"):
            for b0, b1 in ((0, 1), (1, 2), (2, 4)):
                if b0 < 2:
                    column = shared.tile([P, 1], F32, name="fire%d" % b0, offset=SLOT_AT[2 * b0] - 32)
                else:
                    column = keep.tile([P, 2], F32, name="fire%d" % b0)
                nc.sync.dma_start(column[:], fire_rows[:, b0:b1])
                fire_of.extend(column[:, b : b + 1] for b in range(b1 - b0))
        cur_sb = keep.tile([P, PACK, S], F32, name="cur_sb")
        nc.sync.dma_start(cur_sb[:], cur.rearrange("(p t) j -> p t j", t=PACK))

        ident = keep.tile([P, P], F32, name="ident")
        make_identity(nc, ident[:])

        gs = keep.tile([P, S], U8, name="gs", align_bytes=64)
        nc.vector.tensor_copy(gs[:], xs[:].indirect(offs_sb[:]))
        gw = keep.tile([P, S], U32, name="gw", align_bytes=64)
        y = []
        w1_mx = []
        for a0, a1 in ((0, 1), (1, 2), (2, 3), (3, 4)):
            width = (a1 - a0) * P
            if a0 == 1:
                grouped = shared.tile([P, width, PACK], BF16, name="w1_bf%d" % a0, align_bytes=64, offset=24576)
            else:
                grouped = keep.tile([P, width, PACK], BF16, name="w1_bf%d" % a0, align_bytes=64)
            for a in range(a0, a1):
                round_and_interleave(grouped[:, (a - a0) * P : (a - a0 + 1) * P, :], w1_raw[a])
            if a0 == 3:
                codes = shared.tile([P, width], U32, name="w1_codes%d" % a0, align_bytes=64, offset=28672)
            else:
                codes = keep.tile([P, width], U32, name="w1_codes%d" % a0, align_bytes=64)
            scales = keep.tile([P, width], U8, name="w1_scales%d" % a0, align_bytes=64)
            nc.vector.quantize_mx(codes[:].bitcast(FP8X4), scales[:], grouped[:].rearrange("p c t -> p (c t)"))
            for a in range(a0, a1):
                cols = slice((a - a0) * P, (a - a0 + 1) * P)
                w1_mx.append((codes[:, cols], scales[:, cols]))
            if a0 == 0:
                y_a = keep.tile([P, S], F32, name="y0")
                for n in range(2):
                    cols = slice(n * HALF, (n + 1) * HALF)
                    nc.vector.tensor_copy(gw[:, cols], xw[:].indirect(offs_sb[:, cols.start // LIST_ROWS : cols.stop // LIST_ROWS]))
                    bank = psum.tile([P, HALF], F32, name="ybank", tag="acc", bufs=2)
                    nc.tensor.matmul_mx(bank[:], codes[:].bitcast(FP8X4), scales[:], gw[:, cols].bitcast(FP8X4), gs[:, cols], start=True, stop=True)
                    copy = nc.scalar.copy if n else nc.vector.tensor_copy
                    copy(y_a[:, cols], bank[:])
                y.append(y_a)
        on_scalar = {}

        def fetch_on_scalar(a):
            if (a, 1) in ON_SCALAR:
                if a > 1:
                    g = shared.tile([P, LAST * P], F32, name="fetched%d" % a, offset=SLOT_AT[(2 * a + 1) % 4])
                else:
                    g = keep.tile([P, LAST * P], F32, name="fetched%d" % a)
                nc.scalar.activation(g[:], y[a][:].indirect(pos_sb[1][:, 0 : LAST * P // LIST_ROWS]), COPY)
                on_scalar[a] = g

        for a in range(1, QUARTERS):
            codes, scales = w1_mx[a]
            bank = psum.tile([P, S], F32, name="ybank", tag="back" if a < 3 else "acc", bufs=2)
            nc.tensor.matmul_mx(bank[:], codes.bitcast(FP8X4), scales, gw[:].bitcast(FP8X4), gs[:], start=True, stop=True)
            if a < 3:
                y_a = shared.tile([P, S], F32, name="y%d" % a, offset=(0, 2112, 6080)[a])
            else:
                y_a = keep.tile([P, S], F32, name="y%d" % a)
            nc.scalar.copy(y_a[:], bank[:])
            y.append(y_a)
            fetch_on_scalar(a)

        hT_bank = [psum.tile([P, H], F32, name="hT%d" % jb) for jb in range(BLOCKS)]

        def region(jb, a):
            return hT_bank[jb][:, a * P : (a + 1) * P]

        for a in range(QUARTERS - 1):
            add_transposed(region(LAST, a), y[a][:, LAST * P : S], a == 0, False)

        w2_bf = shared.tile([P, PACK, P, PACK], BF16, name="w2_bf", align_bytes=64, offset=28672)
        out_codes = keep.tile([P, S], U32, name="out_codes", align_bytes=64)
        out_scales = keep.tile([P, S], U8, name="out_scales", align_bytes=64)
        out_rows = out_0.rearrange("(p t) j -> p t j", t=PACK)
        out_words = out_1[0].rearrange("p c r -> p (c r)").bitcast(I32)
        hT_bf = [shared.tile([P, H], BF16, name="hT_bf%d" % jb, offset=16384 + 1024 * jb) for jb in range(BLOCKS)]

        def perceive(j0, a, regions, closes):
            width = len(regions) * P
            terms = []
            for d in range(2):
                if j0 == 0 and (a, d) in ON_SCALAR:
                    g = on_scalar[a]
                elif j0 == 0 and a == 0:
                    g = shared.tile([P, width], F32, name="g%d%d" % (a, d), offset=(24576, 4160)[d])
                elif j0 or a >= 2:
                    at = SLOT_AT[(2 * a + d) % 4] - (32 if j0 and a >= 2 and d == 0 else 0)
                    g = shared.tile([P, width], F32, name="g%d_%d%d" % (j0, a, d), offset=at)
                else:
                    g = keep.tile([P, width], F32, name="g", bufs=PRODUCT_SLOTS)
                fetched = y[a][:].indirect(pos_sb[d][:, j0 // LIST_ROWS : (j0 + width) // LIST_ROWS])
                if j0 == 0 and (a, d) in ON_SCALAR:
                    nc.vector.tensor_tensor(g[:], g[:], kern_sb[d][:, 0:width], MULT)
                else:
                    nc.vector.tensor_tensor(g[:], fetched, kern_sb[d][:, j0 : j0 + width], MULT)
                terms.append(g[:])
            for d, term in enumerate(terms):
                for b, target in enumerate(regions):
                    add_transposed(target, term[:, b * P : (b + 1) * P], False, closes and d == 1)


        def activate(jb, source, a0, a1):
            nc.scalar.activation(
                hT_bf[jb][:].rearrange("j (u p e) -> j u p e", u=2, e=2)[:, :, P // PACK * a0 : P // PACK * a1, :],
                source.rearrange("j (p u e) -> j u p e", u=2, e=2),
                RELU,
                scale=fire_of[jb],
            )

        def turn_back(jb):
            words = hT_bf[jb][:].bitcast(F32)
            back = psum.tile([P, 2, P], F32, name="back", tag="back", bufs=2)
            for u in range(2):
                nc.tensor.transpose(back[:, u, :], words[:, u * P : (u + 1) * P], ident[:])
            h_bf = keep.tile([P, P * PACK], BF16, name="h_bf%d" % jb, align_bytes=64)
            copy = nc.vector.tensor_copy if jb in (1, 2) else nc.scalar.copy
            copy(h_bf[:].bitcast(F32).rearrange("p (j u) -> p j u", u=2), back[:].rearrange("p u j -> p j u"))
            return h_bf

        def quantise_h(jb, h_bf):
            h_codes = keep.tile([P, P], U32, name="h_codes%d" % jb, align_bytes=64)
            h_scales = keep.tile([P, P], U8, name="h_scales%d" % jb, align_bytes=64)
            nc.vector.quantize_mx(h_codes[:].bitcast(FP8X4), h_scales[:], h_bf[:])
            return h_codes, h_scales

        def update(jb, h_codes, h_scales):
            cols = slice(jb * P, (jb + 1) * P)
            if jb == 0:
                banks = [psum.tile([P, 2, P], F32, name="rr", tag="acc", bufs=2) for n in range(2)]
                planes = [banks[t // 2][:, t % 2, :] for t in range(PACK)]
            else:
                rr = psum.tile([P, PACK, P], F32, name="hT%d" % (jb - 1))
                planes = [rr[:, t, :] for t in range(PACK)]
            for t in range(PACK):
                m = slice(t % 2 * P, (t % 2 + 1) * P)
                codes, scales = w2_mx[t // 2]
                nc.tensor.matmul_mx(
                    planes[t], codes[:, m].bitcast(FP8X4), scales[:, m], h_codes[:].bitcast(FP8X4), h_scales[:], start=True, stop=True
                )
            new = keep.tile([P, PACK, P], F32, name="new%d" % jb)
            new_bf = keep.tile([P, P, PACK], BF16, name="new_bf%d" % jb, align_bytes=64)
            if jb == LAST:
                for n in range(2):
                    part = slice(n * P // 2, (n + 1) * P // 2)
                    nc.vector.tensor_tensor(new[:, :, part], rr[:, :, part], cur_sb[:, :, cols][:, :, part], ADD)
                nc.sync.dma_start(out_rows[:, :, cols], new[:])
                round_and_interleave(new_bf[:, 0 : P // 2, :], new[:, :, 0 : P // 2])
                nc.vector.tensor_tensor(
                    new_bf[:, P // 2 : P, :].rearrange("p (c i) t -> p c t i", i=4),
                    rr[:, :, P // 2 : P].rearrange("p t (c i) -> p c t i", i=4),
                    cur_sb[:, :, S - P // 2 : S].rearrange("p t (c i) -> p c t i", i=4),
                    ADD,
                )
            elif jb == 0:
                for n in range(2):
                    pair = slice(2 * n, 2 * n + 2)
                    nc.vector.tensor_tensor(new[:, pair, :], banks[n][:], cur_sb[:, pair, cols], ADD)
                    nc.sync.dma_start(out_rows[:, pair, cols], new[:, pair, :])
                round_and_interleave(new_bf[:], new[:])
            else:
                nc.vector.tensor_tensor(new[:], rr[:], cur_sb[:, :, cols], ADD)
                nc.sync.dma_start(out_rows[:, :, cols], new[:])
                round_and_interleave(new_bf[:], new[:])
            nc.vector.quantize_mx(out_codes[:, cols].bitcast(FP8X4), out_scales[:, cols], new_bf[:].rearrange("p c t -> p (c t)"))
            if jb % 2:
                done = slice((jb - 1) * P, (jb + 1) * P)
                nc.sync.dma_start(out_words[:, done], out_codes[:, done].bitcast(I32))

        for a in range(QUARTERS):
            for jb in range(LAST):
                add_transposed(region(jb, a), y[a][:, jb * P : (jb + 1) * P], a == 0, False)
            perceive(0, a, [region(jb, a) for jb in range(LAST)], a == QUARTERS - 1)

        for m0 in range(0, P, P // 4):
            nc.scalar.copy(
                w2_bf[:].rearrange("p t m j -> p m j t")[:, m0 : m0 + P // 4],
                w2_raw[:].rearrange("p j (m t) -> p m j t", t=PACK)[:, m0 : m0 + P // 4],
            )


        h_mx = []
        for jb in range(LAST):
            activate(jb, hT_bank[jb][:], 0, QUARTERS)
            h_mx.append(turn_back(jb))

        for a in range(QUARTERS - 1):
            perceive(LAST * P, a, [region(LAST, a)], a == QUARTERS - 2)
        activate(LAST, hT_bank[LAST][:, 0 : (QUARTERS - 1) * P], 0, QUARTERS - 1)
        spare = psum.tile([P, P], F32, name="hT0")
        add_transposed(spare[:], y[QUARTERS - 1][:, LAST * P : S], True, False)
        perceive(LAST * P, QUARTERS - 1, [spare[:]], True)
        activate(LAST, spare[:], QUARTERS - 1, QUARTERS)
        h_mx.append(turn_back(LAST))
        w2_mx = []
        h_bf = h_mx
        h_mx = []
        for jb in range(BLOCKS):
            if jb < 2:
                codes = shared.tile([P, N // 2], U32, name="w2_codes%d" % jb, align_bytes=64, offset=(SLOT_AT[0] - 1024 + 64, SLOT_AT[2] - 64)[jb])
                scales = keep.tile([P, N // 2], U8, name="w2_scales%d" % jb, align_bytes=64)
                nc.vector.quantize_mx(codes[:].bitcast(FP8X4), scales[:], w2_bf[:, 2 * jb : 2 * jb + 2].rearrange("p t m j -> p (t m j)"))
                w2_mx.append((codes, scales))
            h_mx.append(quantise_h(jb, h_bf[jb]))

        for jb in range(BLOCKS):
            update(jb, *h_mx[jb])
        for q in range(4):
            queue = nc.sync if q % 2 else nc.scalar
            queue.dma_start(out_2[0, PACK * q : PACK * (q + 1), :].bitcast(I32), scale_rows(out_scales, q))
